import numpy as np
import ml_dtypes


def mxq(x, axis, fmt="e4m3"):
    dtype, down = {"e4m3": (ml_dtypes.float8_e4m3fn, 7), "e5m2": (ml_dtypes.float8_e5m2, 14)}[fmt]
    v = np.moveaxis(np.asarray(x, np.float32).astype(ml_dtypes.bfloat16).astype(np.float64), axis, -1)
    blocks = v.reshape(v.shape[:-1] + (-1, 32))
    amax = np.abs(blocks).max(-1, keepdims=True)
    byte = np.maximum(np.where(amax > 0, np.frexp(amax)[1] - 1 + 127, 0) - down, 1)
    scale = np.exp2(byte - 127.0)
    codes = (blocks / scale).astype(np.float32).astype(dtype).astype(np.float64)
    return np.moveaxis((codes * scale).reshape(v.shape), -1, axis)


WIDE = False


def mx_kscale(k):
    if not WIDE:
        return np.ones(k)
    levels = np.array([24, -24, 12, -12, 0])
    if k % 512:
        return np.exp2(np.random.permutation(np.resize(levels, k // 32))).repeat(32)
    a = np.empty((k // 512, 16))
    for p in range(k // 512):
        a[p, :8] = np.random.permutation(np.resize(levels, 8))
        for g in range(8):
            far = levels[np.abs(levels - a[p, g]) >= 10]
            a[p, g + 8] = far[np.random.randint(len(far))]
    return np.exp2(a.ravel()).repeat(32)


def f64(x):
    return np.asarray(x).astype(np.float64)


def striped(idx):
    return np.tile(idx.reshape(-1, 16).T, (8, 1)).astype(np.uint16)


def unstriped(offs):
    return offs[:16].T.reshape(-1).astype(np.int64)


E2M1 = np.array([0.0, 0.5, 1.0, 1.5, 2.0, 3.0, 4.0, 6.0, -0.0, -0.5, -1.0, -1.5, -2.0, -3.0, -4.0, -6.0])


def pack_weight(w, fmt):
    k, n = w.shape
    w = f64(np.asarray(w, np.float32).astype(ml_dtypes.bfloat16)).reshape(k // 32, 32, n)
    amax = np.abs(w).max(1)
    if fmt == "e4m3":
        byte = np.frexp(amax)[1] - 1 + 127 - 7
    else:
        mant, ex = np.frexp(amax / 6.0)
        byte = np.where(mant > 0.5, ex, ex - 1) + 127
    byte = np.clip(np.where(amax > 0, byte, 1), 1, 254)
    scaled = (w * np.exp2(127.0 - byte)[:, None, :]).reshape(k, n).astype(np.float32)
    by_word = np.ascontiguousarray(scaled.reshape(k // 512, 128, 4, n).transpose(0, 1, 3, 2))
    if fmt == "e4m3":
        words = by_word.astype(ml_dtypes.float8_e4m3fn).view(np.uint8)
    else:
        c = by_word.astype(ml_dtypes.float4_e2m1fn).view(np.uint8) & 0xF
        words = (c[..., 0::2] | (c[..., 1::2] << 4)).reshape(k // 512, 128, 2 * n)
    return np.ascontiguousarray(words), np.ascontiguousarray(byte.astype(np.uint8).reshape(k // 512, 16, n))


def unpack_weight(words, scales, fmt):
    g, _, n = scales.shape
    words = np.ascontiguousarray(words).reshape(g, 128, n, -1)
    if fmt == "e4m3":
        vals = words.view(ml_dtypes.float8_e4m3fn).astype(np.float64)
    else:
        nib = np.empty((g, 128, n, 4), np.uint8)
        nib[..., 0::2] = words & 0xF
        nib[..., 1::2] = words >> 4
        vals = E2M1[nib]
    vals = vals * np.repeat(np.exp2(scales.astype(np.float64) - 127.0), 8, axis=1)[..., None]
    return vals.transpose(0, 1, 3, 2).reshape(g * 512, n)


K, R, N, T, J = 512, 512, 256, 4096, 512


def setup_inputs():
    n = np.random.standard_normal
    s = mx_kscale(K)[:, None]
    u = mx_kscale(R)[:, None]
    p_tab = pack_weight(n((K, T)) * s, "e4m3")
    p_w = pack_weight(n((K, R)) / np.sqrt(K) / s * u.T, "e4m3")
    p_wd = pack_weight(n((R, N)) / np.sqrt(R) / u, "e2m1")
    return {
        "tab_words": p_tab[0],
        "tab_scales": p_tab[1],
        "c": (n((K, J)) * s).astype(np.float32),
        "w_words": p_w[0],
        "w_scales": p_w[1],
        "wc": (n((K, R)) / np.sqrt(K) / s * u.T).astype(np.float32),
        "wd_words": p_wd[0],
        "wd_scales": p_wd[1],
        "b": (0.3 * n(N)).astype(np.float32),
        "offs": striped(np.concatenate([np.random.permutation(T)[:J] for _ in range(4)])),
    }


def reference(tab_words, tab_scales, c, w_words, w_scales, wc, wd_words, wd_scales, b, offs):
    idx = unstriped(offs).reshape(4, J)
    tab_ = unpack_weight(tab_words, tab_scales, "e4m3")[:, idx]
    c_ = mxq(f64(c), 0, "e4m3")
    w_ = unpack_weight(w_words, w_scales, "e4m3")
    a0 = w_.T @ tab_[:, 0]
    a1 = w_.T @ tab_[:, 1]
    a2 = w_.T @ tab_[:, 2]
    a3 = w_.T @ tab_[:, 3]
    wc_ = mxq(f64(wc), 0, "e4m3")
    ac = wc_.T @ c_
    h = np.maximum(np.maximum(np.maximum(np.maximum(a0, a1), a2), a3) + ac, 0.0)
    h_ = mxq(h, 0, "e4m3")
    wd_ = unpack_weight(wd_words, wd_scales, "e2m1")
    y = wd_.T @ h_
    return y + f64(b)[:, None]

@@ -1,0 +1,169 @@
+from contextlib import ExitStack
+
+import concourse.mybir as mybir
+
+K, R, N, T, J, G = 512, 512, 256, 4096, 512, 4
+FLOPS = 2 * K * R * J * (G + 1) + 2 * R * N * J
+
+F32 = mybir.dt.float32
+BF16 = mybir.dt.bfloat16
+I32 = mybir.dt.int32
+U32 = mybir.dt.uint32
+U16 = mybir.dt.uint16
+U8 = mybir.dt.uint8
+FP8X4 = mybir.dt.float8_e4m3fn_x4
+FP4X4 = mybir.dt.float4_e2m1fn_x4
+ACT = mybir.ActivationFunctionType
+MAX = mybir.AluOpType.max
+
+P = 128
+PACK = 4
+TILES = J // P
+
+
+def load_scale_rows(nc, plane, rows):
+    for q in range(4):
+        nc.sync.dma_start(out=plane[32 * q : 32 * q + 4, :].bitcast(I32), in_=rows[4 * q : 4 * q + 4, :].bitcast(I32))
+
+
+def round_and_interleave(nc, grouped, raw):
+    nc.scalar.copy(
+        out=grouped.rearrange("p (c i t) -> p c t i", i=4, t=PACK),
+        in_=raw.rearrange("p t (c i) -> p c t i", i=4),
+    )
+
+
+def tile_list_pnet_bias_kernel(
+    tc, tab_words, tab_scales, c, w_words, w_scales, wc, wd_words, wd_scales, b, offs, out
+):
+    nc = tc.nc
+    with ExitStack() as ctx:
+        keep = ctx.enter_context(tc.tile_pool(name="keep", bufs=1))
+        ring = ctx.enter_context(tc.tile_pool(name="ring", bufs=2))
+        loads = ctx.enter_context(tc.tile_pool(name="loads", bufs=1))
+        rounded = ctx.enter_context(tc.tile_pool(name="rounded", bufs=1))
+        psum = ctx.enter_context(tc.psum_pool(name="psum", bufs=1))
+
+        offsets = keep.tile([P, G * J // 16], U16, name="offsets")
+        tab_plane = keep.tile([P, T], U8, name="tab_plane", align_bytes=64)
+        w_plane = keep.tile([P, R], U8, name="w_plane", align_bytes=64)
+        wd_plane = keep.tile([P, N], U8, name="wd_plane", align_bytes=64)
+        diagonal = loads.tile([P, T + PACK * (R + J) + N], F32, name="diagonal", align_bytes=64, offset=0)
+        table = loads.tile([P, T], I32, name="table", align_bytes=64, offset=0)
+        w_codes = keep.tile([P, R], I32, name="w_codes", align_bytes=64)
+        wd_codes = loads.tile([P, 2 * N], U8, name="wd_codes", align_bytes=64, offset=4 * (T + PACK * (R + J)))
+        wc_raw = loads.tile([P, PACK, R], F32, name="wc_raw", align_bytes=64, offset=4 * T)
+        c_raw = [
+            loads.tile([P, PACK, J // 2], F32, name=f"c_raw{h}", align_bytes=64, offset=4 * (T + PACK * R + h * PACK * J // 2))
+            for h in range(2)
+        ]
+        bias = loads.tile([P, N // P], F32, name="bias", align_bytes=64, offset=4 * (T + PACK * (R + J)) + 2 * N)
+        identity = keep.tile([P, P], F32, name="identity", align_bytes=64)
+
+        nc.gpsimd.iota(diagonal[:, :P], [[1, P]], base=0, channel_multiplier=-1, allow_small_or_imprecise_dtypes=True)
+        nc.vector.memset(tab_plane[:].bitcast(I32), 0)
+        nc.vector.memset(w_plane[:].bitcast(I32), 0)
+        nc.vector.tensor_scalar(identity[:], diagonal[:, :P], 0.0, None, op0=mybir.AluOpType.is_equal)
+        nc.vector.memset(wd_plane[:].bitcast(I32), 0)
+
+        nc.sync.dma_start(offsets[:], offs)
+        nc.sync.dma_start(out=w_codes[:], in_=w_words[0].rearrange("p r i -> p (r i)").bitcast(I32))
+        load_scale_rows(nc, tab_plane, tab_scales[0])
+        nc.sync.dma_start(out=table[:], in_=tab_words[0].rearrange("p t i -> p (t i)").bitcast(I32))
+        load_scale_rows(nc, w_plane, w_scales[0])
+        nc.sync.dma_start(out=wc_raw[:], in_=wc.rearrange("(p t) r -> p t r", t=PACK))
+        c_rows = c.rearrange("(p t) j -> p t j", t=PACK)
+        for h in range(2):
+            nc.sync.dma_start(out=c_raw[h][:], in_=c_rows[:, :, h * (J // 2) : (h + 1) * (J // 2)])
+        nc.sync.dma_start(out=wd_codes[:].bitcast(I32), in_=wd_words[0].bitcast(I32))
+        load_scale_rows(nc, wd_plane, wd_scales[0])
+        with nc.allow_non_contiguous_dma(reason="one bias value a partition"):
+            nc.sync.dma_start(out=bias[:], in_=b.rearrange("(h p) -> p h", p=P))
+
+        picked_plane = keep.tile([P, G * J], U8, name="picked_plane", align_bytes=64)
+        nc.vector.tensor_copy(picked_plane[:], tab_plane[:].indirect(offsets[:]))
+        picked = []
+        for g in range(G):
+            words = keep.tile([P, J], U32, name=f"picked{g}", align_bytes=64)
+            nc.vector.tensor_copy(words[:], table[:].bitcast(U32).indirect(offsets[:, g * (J // 16) : (g + 1) * (J // 16)]))
+            picked.append(words)
+
+        def project(codes, plane, moving, moving_plane, bank_index):
+            bank = psum.tile([P, R], F32, name="bank", tag=f"bank{bank_index}")
+            nc.tensor.matmul_mx(
+                out=bank[:], lhsT=codes.bitcast(FP8X4), lhsT_scale=plane,
+                rhs=moving.bitcast(FP8X4), rhs_scale=moving_plane, start=True, stop=True,
+            )
+            return bank[:].rearrange("p (m t) -> p t m", t=PACK)
+
+        def neighbour(g, jt):
+            return project(
+                picked[g][:, jt * P : (jt + 1) * P],
+                picked_plane[:, g * J + jt * P : g * J + (jt + 1) * P],
+                w_codes[:], w_plane[:], jt,
+            )
+
+        pooled = [keep.tile([P, PACK, P], F32, name=f"pooled{jt}", align_bytes=64) for jt in range(TILES)]
+        own = [keep.tile([P, PACK, P], F32, name=f"own{jt}", align_bytes=64) for jt in range(TILES)]
+        for jt in range(TILES):
+            nc.scalar.copy(out=pooled[jt][:], in_=neighbour(0, jt))
+
+        def pool(g, jt):
+            earlier = pooled[jt]
+            if g == 2:
+                pooled[jt] = rounded.tile([P, PACK, P], F32, name=f"pooled_late{jt}", align_bytes=64, offset=jt * 4 * R)
+            nc.vector.tensor_tensor(out=pooled[jt][:], in0=neighbour(g, jt), in1=earlier[:], op=MAX)
+
+        wc_grouped = rounded.tile([P, PACK * R], BF16, name="wc_grouped", align_bytes=64, offset=0)
+        wc_codes = keep.tile([P, R], U32, name="wc_codes", align_bytes=64)
+        wc_plane = keep.tile([P, R], U8, name="wc_plane", align_bytes=64)
+        round_and_interleave(nc, wc_grouped[:], wc_raw[:])
+        nc.vector.quantize_mx(out=wc_codes[:].bitcast(FP8X4), scales=wc_plane[:], in_=wc_grouped[:])
+
+        def own_part(h):
+            c_grouped = rounded.tile([P, PACK * J // 2], BF16, name=f"c_grouped{h}", align_bytes=64, offset=(2 + h) * 4 * R)
+            c_codes = keep.tile([P, J // 2], U32, name=f"c_codes{h}", align_bytes=64)
+            c_plane = keep.tile([P, J // 2], U8, name=f"c_plane{h}", align_bytes=64)
+            round_and_interleave(nc, c_grouped[:], c_raw[h][:])
+            nc.vector.quantize_mx(out=c_codes[:].bitcast(FP8X4), scales=c_plane[:], in_=c_grouped[:])
+            for u in range(2):
+                cols = slice(u * P, (u + 1) * P)
+                sums = project(c_codes[:, cols], c_plane[:, cols], wc_codes[:], wc_plane[:], 4 + u)
+                nc.scalar.copy(out=own[2 * h + u][:], in_=sums)
+
+        out_rows = out.rearrange("(h p) j -> p h j", p=P)
+
+        def second_layer(jt):
+            summed = psum.tile([P, PACK, P], F32, name="summed", tag=f"bank{6 + jt % 2}")
+            for t in range(PACK):
+                nc.tensor.matmul(summed[:, t, :], own[jt][:, t, :], identity[:], start=t == 0, stop=False, is_transpose=True)
+            for t in range(PACK):
+                nc.tensor.matmul(summed[:, t, :], pooled[jt][:, t, :], identity[:], start=False, stop=t == PACK - 1, is_transpose=True)
+            h_grouped = ring.tile([P, P, PACK], BF16, name="h_grouped", align_bytes=64)
+            nc.scalar.activation(out=h_grouped[:], in_=summed[:].rearrange("p t j -> p j t"), func=ACT.Relu)
+            h_codes = ring.tile([P, P], U32, name="h_codes", align_bytes=64)
+            h_plane = ring.tile([P, P], U8, name="h_plane", align_bytes=64)
+            nc.vector.quantize_mx(out=h_codes[:].bitcast(FP8X4), scales=h_plane[:], in_=h_grouped[:].rearrange("p j t -> p (j t)"))
+            y = psum.tile([P, N // P, P], F32, name="y", tag=f"bank{6 + jt % 2}")
+            result = ring.tile([P, N // P, P], F32, name="result")
+            for h in range(N // P):
+                nc.tensor.matmul_mx(
+                    out=y[:, h, :], lhsT=wd_codes[:, 2 * h * P : 2 * (h + 1) * P].bitcast(FP4X4),
+                    lhsT_scale=wd_plane[:, h * P : (h + 1) * P],
+                    rhs=h_codes[:].bitcast(FP8X4), rhs_scale=h_plane[:], start=True, stop=True,
+                )
+            for h in range(N // P):
+                nc.scalar.activation(out=result[:, h, :], in_=y[:, h, :], func=ACT.Identity, bias=bias[:, h : h + 1])
+            nc.sync.dma_start(out=out_rows[:, :, jt * P : (jt + 1) * P], in_=result[:])
+
+        for jt in range(TILES):
+            pool(1, jt)
+        own_part(0)
+        own_part(1)
+        for jt in range(TILES):
+            pool(2, jt)
+            if jt > 0:
+                pool(3, jt - 1)
+                second_layer(jt - 1)
+        pool(3, TILES - 1)
+        second_layer(TILES - 1)

@@ -1,6 +1,7 @@
 from contextlib import ExitStack
 
 import concourse.mybir as mybir
+from concourse.masks import make_identity
 
 K, R, N, T, J, G = 512, 512, 256, 4096, 512, 4
 FLOPS = 2 * K * R * J * (G + 1) + 2 * R * N * J
@@ -39,7 +40,7 @@ def tile_list_pnet_bias_kernel(
     nc = tc.nc
     with ExitStack() as ctx:
         keep = ctx.enter_context(tc.tile_pool(name="keep", bufs=1))
-        ring = ctx.enter_context(tc.tile_pool(name="ring", bufs=2))
+        ring = ctx.enter_context(tc.tile_pool(name="ring", bufs=TILES))
         loads = ctx.enter_context(tc.tile_pool(name="loads", bufs=1))
         rounded = ctx.enter_context(tc.tile_pool(name="rounded", bufs=1))
         psum = ctx.enter_context(tc.psum_pool(name="psum", bufs=1))
@@ -48,7 +49,7 @@ def tile_list_pnet_bias_kernel(
         tab_plane = keep.tile([P, T], U8, name="tab_plane", align_bytes=64)
         w_plane = keep.tile([P, R], U8, name="w_plane", align_bytes=64)
         wd_plane = keep.tile([P, N], U8, name="wd_plane", align_bytes=64)
-        diagonal = loads.tile([P, T + PACK * (R + J) + N], F32, name="diagonal", align_bytes=64, offset=0)
+        zeros = loads.tile([P, T + PACK * (R + J) + N], I32, name="zeros", align_bytes=64, offset=0)
         table = loads.tile([P, T], I32, name="table", align_bytes=64, offset=0)
         w_codes = keep.tile([P, R], I32, name="w_codes", align_bytes=64)
         wd_codes = loads.tile([P, 2 * N], U8, name="wd_codes", align_bytes=64, offset=4 * (T + PACK * (R + J)))
@@ -60,11 +61,11 @@ def tile_list_pnet_bias_kernel(
         bias = loads.tile([P, N // P], F32, name="bias", align_bytes=64, offset=4 * (T + PACK * (R + J)) + 2 * N)
         identity = keep.tile([P, P], F32, name="identity", align_bytes=64)
 
-        nc.gpsimd.iota(diagonal[:, :P], [[1, P]], base=0, channel_multiplier=-1, allow_small_or_imprecise_dtypes=True)
+        make_identity(nc, identity[:])
         nc.vector.memset(tab_plane[:].bitcast(I32), 0)
-        nc.vector.memset(w_plane[:].bitcast(I32), 0)
-        nc.vector.tensor_scalar(identity[:], diagonal[:, :P], 0.0, None, op0=mybir.AluOpType.is_equal)
-        nc.vector.memset(wd_plane[:].bitcast(I32), 0)
+        nc.vector.memset(zeros[:, : R // 4], 0)
+        nc.vector.tensor_copy(w_plane[:].bitcast(I32), zeros[:, : R // 4])
+        nc.vector.tensor_copy(wd_plane[:].bitcast(I32), zeros[:, : N // 4])
 
         nc.sync.dma_start(offsets[:], offs)
         nc.sync.dma_start(out=w_codes[:], in_=w_words[0].rearrange("p r i -> p (r i)").bitcast(I32))
@@ -96,11 +97,12 @@ def tile_list_pnet_bias_kernel(
             )
             return bank[:].rearrange("p (m t) -> p t m", t=PACK)
 
-        def neighbour(g, jt):
+        def neighbour(step, jt):
+            g = (0, 2, 3, 1)[step]
             return project(
                 picked[g][:, jt * P : (jt + 1) * P],
                 picked_plane[:, g * J + jt * P : g * J + (jt + 1) * P],
-                w_codes[:], w_plane[:], jt,
+                w_codes[:], w_plane[:], jt if step < G - 1 else 6 + jt % 2,
             )
 
         pooled = [keep.tile([P, PACK, P], F32, name=f"pooled{jt}", align_bytes=64) for jt in range(TILES)]
@@ -108,11 +110,14 @@ def tile_list_pnet_bias_kernel(
         for jt in range(TILES):
             nc.scalar.copy(out=pooled[jt][:], in_=neighbour(0, jt))
 
+        late = []
+
         def pool(g, jt):
-            earlier = pooled[jt]
             if g == 2:
-                pooled[jt] = rounded.tile([P, PACK, P], F32, name=f"pooled_late{jt}", align_bytes=64, offset=jt * 4 * R)
-            nc.vector.tensor_tensor(out=pooled[jt][:], in0=neighbour(g, jt), in1=earlier[:], op=MAX)
+                late.append(rounded.tile([P, PACK, P], F32, name=f"late{jt}", align_bytes=64, offset=jt * 4 * R))
+            earlier = late[jt] if g == 3 else pooled[jt]
+            target = late[jt] if g == 2 else pooled[jt]
+            nc.vector.tensor_tensor(out=target[:], in0=neighbour(g, jt), in1=earlier[:], op=MAX)
 
         wc_grouped = rounded.tile([P, PACK * R], BF16, name="wc_grouped", align_bytes=64, offset=0)
         wc_codes = keep.tile([P, R], U32, name="wc_codes", align_bytes=64)
@@ -134,36 +139,63 @@ def tile_list_pnet_bias_kernel(
         out_rows = out.rearrange("(h p) j -> p h j", p=P)
 
         def second_layer(jt):
-            summed = psum.tile([P, PACK, P], F32, name="summed", tag=f"bank{6 + jt % 2}")
+            summed = psum.tile([P, PACK, P], F32, name="summed", tag=f"bank{jt}")
             for t in range(PACK):
                 nc.tensor.matmul(summed[:, t, :], own[jt][:, t, :], identity[:], start=t == 0, stop=False, is_transpose=True)
             for t in range(PACK):
                 nc.tensor.matmul(summed[:, t, :], pooled[jt][:, t, :], identity[:], start=False, stop=t == PACK - 1, is_transpose=True)
             h_grouped = ring.tile([P, P, PACK], BF16, name="h_grouped", align_bytes=64)
             nc.scalar.activation(out=h_grouped[:], in_=summed[:].rearrange("p t j -> p j t"), func=ACT.Relu)
-            h_codes = ring.tile([P, P], U32, name="h_codes", align_bytes=64)
+            h_codes = rounded.tile([P, P], U32, name=f"h_codes{jt}", align_bytes=64, offset=min(jt + 2, TILES - 1) * 4 * R + jt * 4 * P)
             h_plane = ring.tile([P, P], U8, name="h_plane", align_bytes=64)
             nc.vector.quantize_mx(out=h_codes[:].bitcast(FP8X4), scales=h_plane[:], in_=h_grouped[:].rearrange("p j t -> p (j t)"))
-            y = psum.tile([P, N // P, P], F32, name="y", tag=f"bank{6 + jt % 2}")
+            return h_codes, h_plane
+
+        def product(operand, h, target):
+            h_codes, h_plane = operand
+            nc.tensor.matmul_mx(
+                out=target, lhsT=wd_codes[:, 2 * h * P : 2 * (h + 1) * P].bitcast(FP4X4),
+                lhsT_scale=wd_plane[:, h * P : (h + 1) * P],
+                rhs=h_codes[:].bitcast(FP8X4), rhs_scale=h_plane[:], start=True, stop=True,
+            )
+
+        def add_bias_scalar(result, y, h):
+            nc.scalar.activation(out=result, in_=y, func=ACT.Identity, bias=bias[:, h : h + 1])
+
+        def add_bias_vector(result, y, h):
+            nc.vector.tensor_scalar(result, y, bias[:, h : h + 1], None, op0=mybir.AluOpType.add)
+
+        def finish(jt, operand, add_bias):
+            y = psum.tile([P, N // P, P], F32, name="y", tag=f"bank{jt}")
             result = ring.tile([P, N // P, P], F32, name="result")
             for h in range(N // P):
-                nc.tensor.matmul_mx(
-                    out=y[:, h, :], lhsT=wd_codes[:, 2 * h * P : 2 * (h + 1) * P].bitcast(FP4X4),
-                    lhsT_scale=wd_plane[:, h * P : (h + 1) * P],
-                    rhs=h_codes[:].bitcast(FP8X4), rhs_scale=h_plane[:], start=True, stop=True,
-                )
+                product(operand, h, y[:, h, :])
             for h in range(N // P):
-                nc.scalar.activation(out=result[:, h, :], in_=y[:, h, :], func=ACT.Identity, bias=bias[:, h : h + 1])
+                add_bias(result[:, h, :], y[:, h, :], h)
             nc.sync.dma_start(out=out_rows[:, :, jt * P : (jt + 1) * P], in_=result[:])
+
+        def finish_last(jt, operand):
+            for h, (add_bias, queue) in enumerate(((add_bias_scalar, nc.scalar), (add_bias_vector, nc.sync))):
+                y = psum.tile([P, P], F32, name="y_half", tag=f"bank{4 + h}")
+                result = ring.tile([P, P], F32, name="result_half")
+                product(operand, h, y[:])
+                add_bias(result[:], y[:], h)
+                queue.dma_start(out=out_rows[:, h, jt * P : (jt + 1) * P], in_=result[:])
 
         for jt in range(TILES):
             pool(1, jt)
         own_part(0)
         own_part(1)
+        operands = []
+        pool(2, 0)
         for jt in range(TILES):
-            pool(2, jt)
-            if jt > 0:
-                pool(3, jt - 1)
-                second_layer(jt - 1)
-        pool(3, TILES - 1)
-        second_layer(TILES - 1)
+            if jt + 1 < TILES:
+                pool(2, jt + 1)
+            pool(3, jt)
+            if jt >= 2:
+                operands.append(second_layer(jt - 2))
+        operands.append(second_layer(2))
+        operands.append(second_layer(3))
+        for jt in range(TILES - 1):
+            finish(jt, operands[jt], add_bias_vector)
+        finish_last(3, operands[3])

@@ -23,12 +23,12 @@ TILES = J // P
 
 
 def load_scale_rows(nc, plane, rows):
-    for q in range(4):
-        nc.sync.dma_start(out=plane[32 * q : 32 * q + 4, :].bitcast(I32), in_=rows[4 * q : 4 * q + 4, :].bitcast(I32))
+    for r in range(4):
+        nc.sync.dma_start(out=plane[r:P:32, :].bitcast(I32), in_=rows[r:16:4, :].bitcast(I32))
 
 
-def round_and_interleave(nc, grouped, raw):
-    nc.scalar.copy(
+def round_and_interleave(copy, grouped, raw):
+    copy(
         out=grouped.rearrange("p (c i t) -> p c t i", i=4, t=PACK),
         in_=raw.rearrange("p t (c i) -> p c t i", i=4),
     )
@@ -51,9 +51,12 @@ def tile_list_pnet_bias_kernel(
         wd_plane = keep.tile([P, N], U8, name="wd_plane", align_bytes=64)
         zeros = loads.tile([P, T + PACK * (R + J) + N], I32, name="zeros", align_bytes=64, offset=0)
         table = loads.tile([P, T], I32, name="table", align_bytes=64, offset=0)
-        w_codes = keep.tile([P, R], I32, name="w_codes", align_bytes=64)
+        w_codes = loads.tile([P, R], I32, name="w_codes", align_bytes=64, offset=4 * T)
         wd_codes = loads.tile([P, 2 * N], U8, name="wd_codes", align_bytes=64, offset=4 * (T + PACK * (R + J)))
-        wc_raw = loads.tile([P, PACK, R], F32, name="wc_raw", align_bytes=64, offset=4 * T)
+        wc_raw = [
+            keep.tile([P, PACK, R // 2], F32, name="wc_raw0", align_bytes=64),
+            loads.tile([P, PACK, R // 2], F32, name="wc_raw1", align_bytes=64, offset=4 * (T + PACK * R // 2)),
+        ]
         c_raw = [
             loads.tile([P, PACK, J // 2], F32, name=f"c_raw{h}", align_bytes=64, offset=4 * (T + PACK * R + h * PACK * J // 2))
             for h in range(2)
@@ -68,11 +71,13 @@ def tile_list_pnet_bias_kernel(
         nc.vector.tensor_copy(wd_plane[:].bitcast(I32), zeros[:, : N // 4])
 
         nc.sync.dma_start(offsets[:], offs)
-        nc.sync.dma_start(out=w_codes[:], in_=w_words[0].rearrange("p r i -> p (r i)").bitcast(I32))
+        wc_rows = wc.rearrange("(p t) r -> p t r", t=PACK)
+        nc.sync.dma_start(out=wc_raw[0][:], in_=wc_rows[:, :, : R // 2])
         load_scale_rows(nc, tab_plane, tab_scales[0])
         nc.sync.dma_start(out=table[:], in_=tab_words[0].rearrange("p t i -> p (t i)").bitcast(I32))
+        nc.sync.dma_start(out=w_codes[:], in_=w_words[0].rearrange("p r i -> p (r i)").bitcast(I32))
         load_scale_rows(nc, w_plane, w_scales[0])
-        nc.sync.dma_start(out=wc_raw[:], in_=wc.rearrange("(p t) r -> p t r", t=PACK))
+        nc.sync.dma_start(out=wc_raw[1][:], in_=wc_rows[:, :, R // 2 :])
         c_rows = c.rearrange("(p t) j -> p t j", t=PACK)
         for h in range(2):
             nc.sync.dma_start(out=c_raw[h][:], in_=c_rows[:, :, h * (J // 2) : (h + 1) * (J // 2)])
@@ -119,22 +124,22 @@ def tile_list_pnet_bias_kernel(
             target = late[jt] if g == 2 else pooled[jt]
             nc.vector.tensor_tensor(out=target[:], in0=neighbour(g, jt), in1=earlier[:], op=MAX)
 
-        wc_grouped = rounded.tile([P, PACK * R], BF16, name="wc_grouped", align_bytes=64, offset=0)
         wc_codes = keep.tile([P, R], U32, name="wc_codes", align_bytes=64)
         wc_plane = keep.tile([P, R], U8, name="wc_plane", align_bytes=64)
-        round_and_interleave(nc, wc_grouped[:], wc_raw[:])
-        nc.vector.quantize_mx(out=wc_codes[:].bitcast(FP8X4), scales=wc_plane[:], in_=wc_grouped[:])
+        for h, copy in enumerate((nc.vector.tensor_copy, nc.scalar.copy)):
+            cols = slice(h * (R // 2), (h + 1) * (R // 2))
+            wc_grouped = keep.tile([P, PACK * R // 2], BF16, name=f"wc_grouped{h}", align_bytes=64)
+            round_and_interleave(copy, wc_grouped[:], wc_raw[h][:])
+            nc.vector.quantize_mx(out=wc_codes[:, cols].bitcast(FP8X4), scales=wc_plane[:, cols], in_=wc_grouped[:])
 
-        def own_part(h):
-            c_grouped = rounded.tile([P, PACK * J // 2], BF16, name=f"c_grouped{h}", align_bytes=64, offset=(2 + h) * 4 * R)
-            c_codes = keep.tile([P, J // 2], U32, name=f"c_codes{h}", align_bytes=64)
-            c_plane = keep.tile([P, J // 2], U8, name=f"c_plane{h}", align_bytes=64)
-            round_and_interleave(nc, c_grouped[:], c_raw[h][:])
+        def own_part(jt):
+            c_grouped = rounded.tile([P, PACK * P], BF16, name=f"c_grouped{jt}", align_bytes=64, offset=jt * 4 * R)
+            c_codes = keep.tile([P, P], U32, name=f"c_codes{jt}", align_bytes=64)
+            c_plane = keep.tile([P, P], U8, name=f"c_plane{jt}", align_bytes=64)
+            round_and_interleave(nc.scalar.copy, c_grouped[:], c_raw[jt // 2][:, :, (jt % 2) * P : (jt % 2 + 1) * P])
             nc.vector.quantize_mx(out=c_codes[:].bitcast(FP8X4), scales=c_plane[:], in_=c_grouped[:])
-            for u in range(2):
-                cols = slice(u * P, (u + 1) * P)
-                sums = project(c_codes[:, cols], c_plane[:, cols], wc_codes[:], wc_plane[:], 4 + u)
-                nc.scalar.copy(out=own[2 * h + u][:], in_=sums)
+            sums = project(c_codes[:], c_plane[:], wc_codes[:], wc_plane[:], 4 + jt % 2)
+            nc.scalar.copy(out=own[jt][:], in_=sums)
 
         out_rows = out.rearrange("(h p) j -> p h j", p=P)
 
@@ -184,8 +189,8 @@ def tile_list_pnet_bias_kernel(
 
         for jt in range(TILES):
             pool(1, jt)
-        own_part(0)
-        own_part(1)
+        for jt in range(TILES):
+            own_part(jt)
         operands = []
         pool(2, 0)
         for jt in range(TILES):

@@ -20,6 +20,7 @@ MAX = mybir.AluOpType.max
 P = 128
 PACK = 4
 TILES = J // P
+FIRST_ROW = P - 16
 
 
 def load_scale_rows(nc, plane, rows):
@@ -46,38 +47,45 @@ def tile_list_pnet_bias_kernel(
         psum = ctx.enter_context(tc.psum_pool(name="psum", bufs=1))
 
         offsets = keep.tile([P, G * J // 16], U16, name="offsets")
-        tab_plane = keep.tile([P, T], U8, name="tab_plane", align_bytes=64)
+        picked_rows = keep.tile([P, G * J], U8, name="picked_rows", align_bytes=64)
+        picked_plane = keep.tile([P, G * J], U8, name="picked_plane", align_bytes=64)
         w_plane = keep.tile([P, R], U8, name="w_plane", align_bytes=64)
-        wd_plane = keep.tile([P, N], U8, name="wd_plane", align_bytes=64)
-        zeros = loads.tile([P, T + PACK * (R + J) + N], I32, name="zeros", align_bytes=64, offset=0)
-        table = loads.tile([P, T], I32, name="table", align_bytes=64, offset=0)
-        w_codes = loads.tile([P, R], I32, name="w_codes", align_bytes=64, offset=4 * T)
-        wd_codes = loads.tile([P, 2 * N], U8, name="wd_codes", align_bytes=64, offset=4 * (T + PACK * (R + J)))
+        zeros = loads.tile([P, PACK * R], I32, name="zeros", align_bytes=64, offset=0)
+        tab_rows = loads.tile([P, T], U8, name="tab_rows", align_bytes=64, offset=4 * PACK * (R + J // 4))
+        table = keep.tile([P, T], I32, name="table", align_bytes=64)
+        w_codes = keep.tile([P, R], I32, name="w_codes", align_bytes=64)
+        between = 4 * PACK * (R + J // 2)
+        wd_codes = loads.tile([P, 2 * N], U8, name="wd_codes", align_bytes=64, offset=between)
+        wd_plane = loads.tile([P, N], U8, name="wd_plane", align_bytes=64, offset=between + 2 * N)
         wc_raw = [
-            keep.tile([P, PACK, R // 2], F32, name="wc_raw0", align_bytes=64),
-            loads.tile([P, PACK, R // 2], F32, name="wc_raw1", align_bytes=64, offset=4 * (T + PACK * R // 2)),
-        ]
-        c_raw = [
-            loads.tile([P, PACK, J // 2], F32, name=f"c_raw{h}", align_bytes=64, offset=4 * (T + PACK * R + h * PACK * J // 2))
+            loads.tile([P, PACK, R // 2], F32, name=f"wc_raw{h}", align_bytes=64, offset=4 * h * PACK * R // 2)
             for h in range(2)
         ]
-        bias = loads.tile([P, N // P], F32, name="bias", align_bytes=64, offset=4 * (T + PACK * (R + J)) + 2 * N)
+        c_raw = [
+            loads.tile([P, PACK, J // 2], F32, name=f"c_raw{h}", align_bytes=64, offset=4 * PACK * R + h * (4 * PACK * J // 2 + 4 * N))
+            for h in range(2)
+        ]
+        bias = loads.tile([P, N // P], F32, name="bias", align_bytes=64, offset=between + 3 * N)
         identity = keep.tile([P, P], F32, name="identity", align_bytes=64)
 
-        make_identity(nc, identity[:])
-        nc.vector.memset(tab_plane[:].bitcast(I32), 0)
         nc.vector.memset(zeros[:, : R // 4], 0)
         nc.vector.tensor_copy(w_plane[:].bitcast(I32), zeros[:, : R // 4])
-        nc.vector.tensor_copy(wd_plane[:].bitcast(I32), zeros[:, : N // 4])
+        nc.vector.memset(tab_rows[:FIRST_ROW, :].bitcast(I32), 0)
+        nc.vector.memset(picked_plane[:].bitcast(I32), 0)
+        make_identity(nc, identity[:])
 
         nc.sync.dma_start(offsets[:], offs)
+        nc.sync.dma_start(out=tab_rows[FIRST_ROW:, :].bitcast(I32), in_=tab_scales[0].bitcast(I32))
         wc_rows = wc.rearrange("(p t) r -> p t r", t=PACK)
-        nc.sync.dma_start(out=wc_raw[0][:], in_=wc_rows[:, :, : R // 2])
-        load_scale_rows(nc, tab_plane, tab_scales[0])
         nc.sync.dma_start(out=table[:], in_=tab_words[0].rearrange("p t i -> p (t i)").bitcast(I32))
         nc.sync.dma_start(out=w_codes[:], in_=w_words[0].rearrange("p r i -> p (r i)").bitcast(I32))
         load_scale_rows(nc, w_plane, w_scales[0])
-        nc.sync.dma_start(out=wc_raw[1][:], in_=wc_rows[:, :, R // 2 :])
+        for h in range(2):
+            nc.sync.dma_start(out=wc_raw[h][:], in_=wc_rows[:, :, h * (R // 2) : (h + 1) * (R // 2)])
+        nc.vector.tensor_copy(picked_rows[:], tab_rows[:].indirect(offsets[:]))
+        for r in range(4):
+            nc.sync.dma_start(out=picked_plane[r:P:32, :].bitcast(I32), in_=picked_rows[FIRST_ROW + r : P : 4, :].bitcast(I32))
+        nc.gpsimd.memset(wd_plane[:].bitcast(I32), 0)
         c_rows = c.rearrange("(p t) j -> p t j", t=PACK)
         for h in range(2):
             nc.sync.dma_start(out=c_raw[h][:], in_=c_rows[:, :, h * (J // 2) : (h + 1) * (J // 2)])
@@ -85,9 +93,6 @@ def tile_list_pnet_bias_kernel(
         load_scale_rows(nc, wd_plane, wd_scales[0])
         with nc.allow_non_contiguous_dma(reason="one bias value a partition"):
             nc.sync.dma_start(out=bias[:], in_=b.rearrange("(h p) -> p h", p=P))
-
-        picked_plane = keep.tile([P, G * J], U8, name="picked_plane", align_bytes=64)
-        nc.vector.tensor_copy(picked_plane[:], tab_plane[:].indirect(offsets[:]))
         picked = []
         for g in range(G):
             words = keep.tile([P, J], U32, name=f"picked{g}", align_bytes=64)
@@ -126,7 +131,7 @@ def tile_list_pnet_bias_kernel(
 
         wc_codes = keep.tile([P, R], U32, name="wc_codes", align_bytes=64)
         wc_plane = keep.tile([P, R], U8, name="wc_plane", align_bytes=64)
-        for h, copy in enumerate((nc.vector.tensor_copy, nc.scalar.copy)):
+        for h, copy in enumerate((nc.scalar.copy, nc.scalar.copy)):
             cols = slice(h * (R // 2), (h + 1) * (R // 2))
             wc_grouped = keep.tile([P, PACK * R // 2], BF16, name=f"wc_grouped{h}", align_bytes=64)
             round_and_interleave(copy, wc_grouped[:], wc_raw[h][:])

@@ -1,7 +1,6 @@
 from contextlib import ExitStack
 
 import concourse.mybir as mybir
-from concourse.masks import make_identity
 
 K, R, N, T, J, G = 512, 512, 256, 4096, 512, 4
 FLOPS = 2 * K * R * J * (G + 1) + 2 * R * N * J
@@ -16,11 +15,15 @@ FP8X4 = mybir.dt.float8_e4m3fn_x4
 FP4X4 = mybir.dt.float4_e2m1fn_x4
 ACT = mybir.ActivationFunctionType
 MAX = mybir.AluOpType.max
+MULT = mybir.AluOpType.mult
+ADD = mybir.AluOpType.add
 
 P = 128
 PACK = 4
 TILES = J // P
 FIRST_ROW = P - 16
+ADDED = (0, 1)
+FOLDED = (2, 3)
 
 
 def load_scale_rows(nc, plane, rows):
@@ -28,11 +31,8 @@ def load_scale_rows(nc, plane, rows):
         nc.sync.dma_start(out=plane[r:P:32, :].bitcast(I32), in_=rows[r:16:4, :].bitcast(I32))
 
 
-def round_and_interleave(copy, grouped, raw):
-    copy(
-        out=grouped.rearrange("p (c i t) -> p c t i", i=4, t=PACK),
-        in_=raw.rearrange("p t (c i) -> p c t i", i=4),
-    )
+def columns(tile, width=P):
+    return slice(tile * width, (tile + 1) * width)
 
 
 def tile_list_pnet_bias_kernel(
@@ -41,7 +41,6 @@ def tile_list_pnet_bias_kernel(
     nc = tc.nc
     with ExitStack() as ctx:
         keep = ctx.enter_context(tc.tile_pool(name="keep", bufs=1))
-        ring = ctx.enter_context(tc.tile_pool(name="ring", bufs=TILES))
         loads = ctx.enter_context(tc.tile_pool(name="loads", bufs=1))
         rounded = ctx.enter_context(tc.tile_pool(name="rounded", bufs=1))
         psum = ctx.enter_context(tc.psum_pool(name="psum", bufs=1))
@@ -50,13 +49,14 @@ def tile_list_pnet_bias_kernel(
         picked_rows = keep.tile([P, G * J], U8, name="picked_rows", align_bytes=64)
         picked_plane = keep.tile([P, G * J], U8, name="picked_plane", align_bytes=64)
         w_plane = keep.tile([P, R], U8, name="w_plane", align_bytes=64)
-        zeros = loads.tile([P, PACK * R], I32, name="zeros", align_bytes=64, offset=0)
-        tab_rows = loads.tile([P, T], U8, name="tab_rows", align_bytes=64, offset=4 * PACK * (R + J // 4))
         table = keep.tile([P, T], I32, name="table", align_bytes=64)
         w_codes = keep.tile([P, R], I32, name="w_codes", align_bytes=64)
+        zeros = loads.tile([P, PACK * R], I32, name="zeros", align_bytes=64, offset=0)
+        tab_rows = loads.tile([P, T], U8, name="tab_rows", align_bytes=64, offset=4 * PACK * (R + J // 4))
         between = 4 * PACK * (R + J // 2)
         wd_codes = loads.tile([P, 2 * N], U8, name="wd_codes", align_bytes=64, offset=between)
         wd_plane = loads.tile([P, N], U8, name="wd_plane", align_bytes=64, offset=between + 2 * N)
+        bias = loads.tile([P, N // P], F32, name="bias", align_bytes=64, offset=between + 3 * N)
         wc_raw = [
             loads.tile([P, PACK, R // 2], F32, name=f"wc_raw{h}", align_bytes=64, offset=4 * h * PACK * R // 2)
             for h in range(2)
@@ -65,147 +65,146 @@ def tile_list_pnet_bias_kernel(
             loads.tile([P, PACK, J // 2], F32, name=f"c_raw{h}", align_bytes=64, offset=4 * PACK * R + h * (4 * PACK * J // 2 + 4 * N))
             for h in range(2)
         ]
-        bias = loads.tile([P, N // P], F32, name="bias", align_bytes=64, offset=between + 3 * N)
-        identity = keep.tile([P, P], F32, name="identity", align_bytes=64)
 
         nc.vector.memset(zeros[:, : R // 4], 0)
         nc.vector.tensor_copy(w_plane[:].bitcast(I32), zeros[:, : R // 4])
         nc.vector.memset(tab_rows[:FIRST_ROW, :].bitcast(I32), 0)
         nc.vector.memset(picked_plane[:].bitcast(I32), 0)
-        make_identity(nc, identity[:])
 
         nc.sync.dma_start(offsets[:], offs)
         nc.sync.dma_start(out=tab_rows[FIRST_ROW:, :].bitcast(I32), in_=tab_scales[0].bitcast(I32))
-        wc_rows = wc.rearrange("(p t) r -> p t r", t=PACK)
         nc.sync.dma_start(out=table[:], in_=tab_words[0].rearrange("p t i -> p (t i)").bitcast(I32))
         nc.sync.dma_start(out=w_codes[:], in_=w_words[0].rearrange("p r i -> p (r i)").bitcast(I32))
         load_scale_rows(nc, w_plane, w_scales[0])
+        wc_rows = wc.rearrange("(p t) r -> p t r", t=PACK)
         for h in range(2):
-            nc.sync.dma_start(out=wc_raw[h][:], in_=wc_rows[:, :, h * (R // 2) : (h + 1) * (R // 2)])
+            nc.sync.dma_start(out=wc_raw[h][:], in_=wc_rows[:, :, columns(h, R // 2)])
+
         nc.vector.tensor_copy(picked_rows[:], tab_rows[:].indirect(offsets[:]))
         for r in range(4):
             nc.sync.dma_start(out=picked_plane[r:P:32, :].bitcast(I32), in_=picked_rows[FIRST_ROW + r : P : 4, :].bitcast(I32))
         nc.gpsimd.memset(wd_plane[:].bitcast(I32), 0)
         c_rows = c.rearrange("(p t) j -> p t j", t=PACK)
-        for h in range(2):
-            nc.sync.dma_start(out=c_raw[h][:], in_=c_rows[:, :, h * (J // 2) : (h + 1) * (J // 2)])
+        for h in (1, 0):
+            nc.sync.dma_start(out=c_raw[h][:], in_=c_rows[:, :, columns(h, J // 2)])
         nc.sync.dma_start(out=wd_codes[:].bitcast(I32), in_=wd_words[0].bitcast(I32))
         load_scale_rows(nc, wd_plane, wd_scales[0])
         with nc.allow_non_contiguous_dma(reason="one bias value a partition"):
             nc.sync.dma_start(out=bias[:], in_=b.rearrange("(h p) -> p h", p=P))
+
         picked = []
         for g in range(G):
             words = keep.tile([P, J], U32, name=f"picked{g}", align_bytes=64)
-            nc.vector.tensor_copy(words[:], table[:].bitcast(U32).indirect(offsets[:, g * (J // 16) : (g + 1) * (J // 16)]))
+            nc.vector.tensor_copy(words[:], table[:].bitcast(U32).indirect(offsets[:, columns(g, J // 16)]))
             picked.append(words)
 
-        def project(codes, plane, moving, moving_plane, bank_index):
-            bank = psum.tile([P, R], F32, name="bank", tag=f"bank{bank_index}")
-            nc.tensor.matmul_mx(
-                out=bank[:], lhsT=codes.bitcast(FP8X4), lhsT_scale=plane,
-                rhs=moving.bitcast(FP8X4), rhs_scale=moving_plane, start=True, stop=True,
-            )
-            return bank[:].rearrange("p (m t) -> p t m", t=PACK)
+        w_dealt = keep.tile([P, R], I32, name="w_dealt", align_bytes=64)
+        w_dealt_plane = keep.tile([P, R], U8, name="w_dealt_plane", align_bytes=64)
+        for dealt, source in ((w_dealt, w_codes), (w_dealt_plane, w_plane)):
+            nc.gpsimd.tensor_copy(dealt[:].rearrange("p (t m) -> p t m", t=PACK), source[:].rearrange("p (m t) -> p t m", t=PACK))
 
-        def neighbour(step, jt):
-            g = (0, 2, 3, 1)[step]
-            return project(
-                picked[g][:, jt * P : (jt + 1) * P],
-                picked_plane[:, g * J + jt * P : g * J + (jt + 1) * P],
-                w_codes[:], w_plane[:], jt if step < G - 1 else 6 + jt % 2,
-            )
-
-        pooled = [keep.tile([P, PACK, P], F32, name=f"pooled{jt}", align_bytes=64) for jt in range(TILES)]
-        own = [keep.tile([P, PACK, P], F32, name=f"own{jt}", align_bytes=64) for jt in range(TILES)]
-        for jt in range(TILES):
-            nc.scalar.copy(out=pooled[jt][:], in_=neighbour(0, jt))
-
-        late = []
-
-        def pool(g, jt):
-            if g == 2:
-                late.append(rounded.tile([P, PACK, P], F32, name=f"late{jt}", align_bytes=64, offset=jt * 4 * R))
-            earlier = late[jt] if g == 3 else pooled[jt]
-            target = late[jt] if g == 2 else pooled[jt]
-            nc.vector.tensor_tensor(out=target[:], in0=neighbour(g, jt), in1=earlier[:], op=MAX)
-
+        wc_grouped = keep.tile([P, PACK * R], BF16, name="wc_grouped", align_bytes=64)
         wc_codes = keep.tile([P, R], U32, name="wc_codes", align_bytes=64)
         wc_plane = keep.tile([P, R], U8, name="wc_plane", align_bytes=64)
-        for h, copy in enumerate((nc.scalar.copy, nc.scalar.copy)):
-            cols = slice(h * (R // 2), (h + 1) * (R // 2))
-            wc_grouped = keep.tile([P, PACK * R // 2], BF16, name=f"wc_grouped{h}", align_bytes=64)
-            round_and_interleave(copy, wc_grouped[:], wc_raw[h][:])
-            nc.vector.quantize_mx(out=wc_codes[:, cols].bitcast(FP8X4), scales=wc_plane[:, cols], in_=wc_grouped[:])
+        c_codes = keep.tile([P, J], U32, name="c_codes", align_bytes=64)
+        c_plane = keep.tile([P, J], U8, name="c_plane", align_bytes=64)
+        wc_dealt = wc_grouped[:].rearrange("p (t h m i) -> p h m i t", t=PACK, h=2, i=PACK)
+        for h in range(2):
+            nc.scalar.copy(out=wc_dealt[:, h], in_=wc_raw[h][:].rearrange("p i (m t) -> p m i t", t=PACK))
 
-        def own_part(jt):
-            c_grouped = rounded.tile([P, PACK * P], BF16, name=f"c_grouped{jt}", align_bytes=64, offset=jt * 4 * R)
-            c_codes = keep.tile([P, P], U32, name=f"c_codes{jt}", align_bytes=64)
-            c_plane = keep.tile([P, P], U8, name=f"c_plane{jt}", align_bytes=64)
-            round_and_interleave(nc.scalar.copy, c_grouped[:], c_raw[jt // 2][:, :, (jt % 2) * P : (jt % 2 + 1) * P])
-            nc.vector.quantize_mx(out=c_codes[:].bitcast(FP8X4), scales=c_plane[:], in_=c_grouped[:])
-            sums = project(c_codes[:], c_plane[:], wc_codes[:], wc_plane[:], 4 + jt % 2)
-            nc.scalar.copy(out=own[jt][:], in_=sums)
+        def sums(index, jt, g=None, with_own=False):
+            bank = psum.tile([P, PACK, P], F32, name="bank", tag=f"bank{index}")
+            passes = []
+            if g is not None:
+                passes.append((w_dealt, w_dealt_plane, picked[g][:, columns(jt)], picked_plane[:, columns(g * TILES + jt)]))
+            if with_own:
+                passes.append((wc_codes, wc_plane, c_codes[:, columns(jt)], c_plane[:, columns(jt)]))
+            for n, (codes, plane, moving, moving_plane) in enumerate(passes):
+                for t in range(PACK):
+                    nc.tensor.matmul_mx(
+                        out=bank[:, t, :], lhsT=codes[:, columns(t)].bitcast(FP8X4), lhsT_scale=plane[:, columns(t)],
+                        rhs=moving.bitcast(FP8X4), rhs_scale=moving_plane,
+                        start=n == 0 and t == 0, stop=n == len(passes) - 1 and t == PACK - 1,
+                    )
+            return bank[:].rearrange("p t j -> p j t")
+
+        first = {}
+        for jt in FOLDED + ADDED:
+            first[jt] = keep.tile([P, P, PACK], F32, name=f"first{jt}", align_bytes=64)
+            nc.scalar.copy(out=first[jt][:], in_=sums(jt, jt, g=0))
+        nc.vector.quantize_mx(out=wc_codes[:].bitcast(FP8X4), scales=wc_plane[:], in_=wc_grouped[:])
+
+        def maximum(target, earlier, g, jt):
+            nc.vector.tensor_tensor(out=target[:], in0=sums((g % 2) * TILES + jt, jt, g=g), in1=earlier[:], op=MAX)
+
+        for g in (1, 2):
+            for jt in FOLDED:
+                maximum(first[jt], first[jt], g, jt)
+
+        c_grouped = rounded.tile([P, PACK * J], BF16, name="c_grouped", align_bytes=64, offset=0)
+        for jt in FOLDED + ADDED:
+            nc.gpsimd.tensor_scalar(
+                c_grouped[:, columns(jt, PACK * P)].rearrange("p (j t) -> p j t", t=PACK),
+                c_raw[jt // 2][:, :, columns(jt % 2)].rearrange("p t j -> p j t"), 1.0, 0.0, op0=MULT, op1=ADD,
+            )
+        nc.vector.quantize_mx(out=c_codes[:].bitcast(FP8X4), scales=c_plane[:], in_=c_grouped[:])
+
+        three = {}
+        for jt in FOLDED:
+            own = keep.tile([P, P, PACK], F32, name=f"own{jt}", align_bytes=64)
+            nc.scalar.copy(out=own[:], in_=sums(TILES + jt, jt, with_own=True))
+            three[jt] = keep.tile([P, P, PACK], BF16, name=f"three{jt}", align_bytes=64)
+            nc.gpsimd.tensor_tensor(out=three[jt][:], in0=first[jt][:], in1=own[:], op=ADD)
+
+        pooled = {jt: rounded.tile([P, P, PACK], F32, name=f"pooled{jt}", align_bytes=64, offset=jt * 4 * R) for jt in ADDED}
+        for g in (1, 2, 3):
+            for jt in ADDED:
+                maximum(pooled[jt], first[jt] if g == 1 else pooled[jt], g, jt)
+
+        h_grouped = keep.tile([P, TILES, P, PACK], BF16, name="h_grouped", align_bytes=64)
+        h_codes = keep.tile([P, J], U32, name="h_codes", align_bytes=64)
+        h_plane = keep.tile([P, J], U8, name="h_plane", align_bytes=64)
+        for jt in ADDED:
+            signed = keep.tile([P, P, PACK], BF16, name=f"signed{jt}", align_bytes=64)
+            nc.vector.tensor_tensor(out=signed[:], in0=sums(FOLDED[jt], jt, with_own=True), in1=pooled[jt][:], op=ADD)
+            nc.scalar.activation(out=h_grouped[:, jt], in_=signed[:], func=ACT.Relu)
+
+        def last_maximum(jt):
+            nc.vector.scalar_tensor_tensor(
+                out=h_grouped[:, jt], in0=sums(TILES + jt, jt, g=3, with_own=True), scalar=0.0, in1=three[jt][:], op0=MAX, op1=MAX,
+            )
+
+        def quantise(first_tile, count):
+            cols = slice(first_tile * P, (first_tile + count) * P)
+            nc.vector.quantize_mx(
+                out=h_codes[:, cols].bitcast(FP8X4), scales=h_plane[:, cols],
+                in_=h_grouped[:, first_tile : first_tile + count].rearrange("p a j t -> p (a j t)"),
+            )
 
         out_rows = out.rearrange("(h p) j -> p h j", p=P)
-
-        def second_layer(jt):
-            summed = psum.tile([P, PACK, P], F32, name="summed", tag=f"bank{jt}")
-            for t in range(PACK):
-                nc.tensor.matmul(summed[:, t, :], own[jt][:, t, :], identity[:], start=t == 0, stop=False, is_transpose=True)
-            for t in range(PACK):
-                nc.tensor.matmul(summed[:, t, :], pooled[jt][:, t, :], identity[:], start=False, stop=t == PACK - 1, is_transpose=True)
-            h_grouped = ring.tile([P, P, PACK], BF16, name="h_grouped", align_bytes=64)
-            nc.scalar.activation(out=h_grouped[:], in_=summed[:].rearrange("p t j -> p j t"), func=ACT.Relu)
-            h_codes = rounded.tile([P, P], U32, name=f"h_codes{jt}", align_bytes=64, offset=min(jt + 2, TILES - 1) * 4 * R + jt * 4 * P)
-            h_plane = ring.tile([P, P], U8, name="h_plane", align_bytes=64)
-            nc.vector.quantize_mx(out=h_codes[:].bitcast(FP8X4), scales=h_plane[:], in_=h_grouped[:].rearrange("p j t -> p (j t)"))
-            return h_codes, h_plane
-
-        def product(operand, h, target):
-            h_codes, h_plane = operand
-            nc.tensor.matmul_mx(
-                out=target, lhsT=wd_codes[:, 2 * h * P : 2 * (h + 1) * P].bitcast(FP4X4),
-                lhsT_scale=wd_plane[:, h * P : (h + 1) * P],
-                rhs=h_codes[:].bitcast(FP8X4), rhs_scale=h_plane[:], start=True, stop=True,
-            )
 
         def add_bias_scalar(result, y, h):
             nc.scalar.activation(out=result, in_=y, func=ACT.Identity, bias=bias[:, h : h + 1])
 
         def add_bias_vector(result, y, h):
-            nc.vector.tensor_scalar(result, y, bias[:, h : h + 1], None, op0=mybir.AluOpType.add)
+            nc.vector.tensor_scalar(result, y, bias[:, h : h + 1], None, op0=ADD)
 
-        def finish(jt, operand, add_bias):
-            y = psum.tile([P, N // P, P], F32, name="y", tag=f"bank{jt}")
-            result = ring.tile([P, N // P, P], F32, name="result")
-            for h in range(N // P):
-                product(operand, h, y[:, h, :])
-            for h in range(N // P):
-                add_bias(result[:, h, :], y[:, h, :], h)
-            nc.sync.dma_start(out=out_rows[:, :, jt * P : (jt + 1) * P], in_=result[:])
+        def finish(pair, banks, adders, queues):
+            cols = columns(pair, 2 * P)
+            for h in range(2):
+                y = psum.tile([P, 2 * P], F32, name="bank", tag=f"bank{banks[h]}")
+                nc.tensor.matmul_mx(
+                    out=y[:], lhsT=wd_codes[:, columns(h, 2 * P)].bitcast(FP4X4), lhsT_scale=wd_plane[:, columns(h)],
+                    rhs=h_codes[:, cols].bitcast(FP8X4), rhs_scale=h_plane[:, cols], start=True, stop=True,
+                )
+                result = keep.tile([P, 2 * P], F32, name=f"result{pair}{h}")
+                adders[h](result[:], y[:], h)
+                queues[h].dma_start(out=out_rows[:, h, cols], in_=result[:])
 
-        def finish_last(jt, operand):
-            for h, (add_bias, queue) in enumerate(((add_bias_scalar, nc.scalar), (add_bias_vector, nc.sync))):
-                y = psum.tile([P, P], F32, name="y_half", tag=f"bank{4 + h}")
-                result = ring.tile([P, P], F32, name="result_half")
-                product(operand, h, y[:])
-                add_bias(result[:], y[:], h)
-                queue.dma_start(out=out_rows[:, h, jt * P : (jt + 1) * P], in_=result[:])
-
-        for jt in range(TILES):
-            pool(1, jt)
-        for jt in range(TILES):
-            own_part(jt)
-        operands = []
-        pool(2, 0)
-        for jt in range(TILES):
-            if jt + 1 < TILES:
-                pool(2, jt + 1)
-            pool(3, jt)
-            if jt >= 2:
-                operands.append(second_layer(jt - 2))
-        operands.append(second_layer(2))
-        operands.append(second_layer(3))
-        for jt in range(TILES - 1):
-            finish(jt, operands[jt], add_bias_vector)
-        finish_last(3, operands[3])
+        last_maximum(2)
+        quantise(0, 2)
+        last_maximum(3)
+        quantise(2, 1)
+        quantise(3, 1)
+        finish(0, (0, 1), (add_bias_scalar, add_bias_scalar), (nc.sync, nc.sync))
+        finish(1, (4, 5), (add_bias_scalar, add_bias_vector), (nc.scalar, nc.sync))

@@ -15,7 +15,6 @@ FP8X4 = mybir.dt.float8_e4m3fn_x4
 FP4X4 = mybir.dt.float4_e2m1fn_x4
 ACT = mybir.ActivationFunctionType
 MAX = mybir.AluOpType.max
-MULT = mybir.AluOpType.mult
 ADD = mybir.AluOpType.add
 
 P = 128
@@ -43,14 +42,15 @@ def tile_list_pnet_bias_kernel(
         keep = ctx.enter_context(tc.tile_pool(name="keep", bufs=1))
         loads = ctx.enter_context(tc.tile_pool(name="loads", bufs=1))
         rounded = ctx.enter_context(tc.tile_pool(name="rounded", bufs=1))
+        dealt_from = ctx.enter_context(tc.tile_pool(name="dealt_from", bufs=1))
         psum = ctx.enter_context(tc.psum_pool(name="psum", bufs=1))
 
         offsets = keep.tile([P, G * J // 16], U16, name="offsets")
         picked_rows = keep.tile([P, G * J], U8, name="picked_rows", align_bytes=64)
         picked_plane = keep.tile([P, G * J], U8, name="picked_plane", align_bytes=64)
-        w_plane = keep.tile([P, R], U8, name="w_plane", align_bytes=64)
+        w_plane = dealt_from.tile([P, R], U8, name="w_plane", align_bytes=64, offset=4 * R)
         table = keep.tile([P, T], I32, name="table", align_bytes=64)
-        w_codes = keep.tile([P, R], I32, name="w_codes", align_bytes=64)
+        w_codes = dealt_from.tile([P, R], I32, name="w_codes", align_bytes=64, offset=0)
         zeros = loads.tile([P, PACK * R], I32, name="zeros", align_bytes=64, offset=0)
         tab_rows = loads.tile([P, T], U8, name="tab_rows", align_bytes=64, offset=4 * PACK * (R + J // 4))
         between = 4 * PACK * (R + J // 2)
@@ -92,16 +92,16 @@ def tile_list_pnet_bias_kernel(
         with nc.allow_non_contiguous_dma(reason="one bias value a partition"):
             nc.sync.dma_start(out=bias[:], in_=b.rearrange("(h p) -> p h", p=P))
 
-        picked = []
-        for g in range(G):
-            words = keep.tile([P, J], U32, name=f"picked{g}", align_bytes=64)
-            nc.vector.tensor_copy(words[:], table[:].bitcast(U32).indirect(offsets[:, columns(g, J // 16)]))
-            picked.append(words)
-
         w_dealt = keep.tile([P, R], I32, name="w_dealt", align_bytes=64)
         w_dealt_plane = keep.tile([P, R], U8, name="w_dealt_plane", align_bytes=64)
         for dealt, source in ((w_dealt, w_codes), (w_dealt_plane, w_plane)):
-            nc.gpsimd.tensor_copy(dealt[:].rearrange("p (t m) -> p t m", t=PACK), source[:].rearrange("p (m t) -> p t m", t=PACK))
+            nc.vector.tensor_copy(dealt[:].rearrange("p (t m) -> p t m", t=PACK), source[:].rearrange("p (m t) -> p t m", t=PACK))
+
+        picked_first = rounded.tile([P, J], U32, name="picked_first", align_bytes=64, offset=2 * R)
+        picked_rest = dealt_from.tile([P, (G - 1) * J], U32, name="picked_rest", align_bytes=64, offset=0)
+        picked = [picked_first[:]] + [picked_rest[:, columns(g, J)] for g in range(G - 1)]
+        for g in range(G):
+            nc.vector.tensor_copy(picked[g], table[:].bitcast(U32).indirect(offsets[:, columns(g, J // 16)]))
 
         wc_grouped = keep.tile([P, PACK * R], BF16, name="wc_grouped", align_bytes=64)
         wc_codes = keep.tile([P, R], U32, name="wc_codes", align_bytes=64)
@@ -128,10 +128,29 @@ def tile_list_pnet_bias_kernel(
                     )
             return bank[:].rearrange("p t j -> p j t")
 
-        first = {}
-        for jt in FOLDED + ADDED:
-            first[jt] = keep.tile([P, P, PACK], F32, name=f"first{jt}", align_bytes=64)
-            nc.scalar.copy(out=first[jt][:], in_=sums(jt, jt, g=0))
+        first = {jt: keep.tile([P, P, PACK], F32, name=f"first{jt}", align_bytes=64) for jt in range(TILES)}
+        first_sums = {jt: sums(jt, jt, g=0) for jt in FOLDED + ADDED}
+        c_grouped = [
+            keep.tile([P, PACK * J // 2], BF16, name="c_grouped0", align_bytes=64),
+            rounded.tile([P, PACK * J // 2], BF16, name="c_grouped1", align_bytes=64, offset=2 * R),
+        ]
+
+        def round_c(jt):
+            nc.scalar.copy(
+                out=c_grouped[jt // 2][:, columns(jt % 2, PACK * P)].rearrange("p (j i t) -> p j t i", i=4, t=PACK),
+                in_=c_raw[jt // 2][:, :, columns(jt % 2)].rearrange("p t (j i) -> p j t i", i=4),
+            )
+
+        def quantise_c(half):
+            cols = columns(half, J // 2)
+            nc.vector.quantize_mx(out=c_codes[:, cols].bitcast(FP8X4), scales=c_plane[:, cols], in_=c_grouped[half][:])
+
+        for jt in FOLDED:
+            nc.scalar.copy(out=first[jt][:], in_=first_sums[jt])
+        for jt in FOLDED:
+            round_c(jt)
+        for jt in ADDED:
+            nc.scalar.copy(out=first[jt][:], in_=first_sums[jt])
         nc.vector.quantize_mx(out=wc_codes[:].bitcast(FP8X4), scales=wc_plane[:], in_=wc_grouped[:])
 
         def maximum(target, earlier, g, jt):
@@ -141,13 +160,7 @@ def tile_list_pnet_bias_kernel(
             for jt in FOLDED:
                 maximum(first[jt], first[jt], g, jt)
 
-        c_grouped = rounded.tile([P, PACK * J], BF16, name="c_grouped", align_bytes=64, offset=0)
-        for jt in FOLDED + ADDED:
-            nc.gpsimd.tensor_scalar(
-                c_grouped[:, columns(jt, PACK * P)].rearrange("p (j t) -> p j t", t=PACK),
-                c_raw[jt // 2][:, :, columns(jt % 2)].rearrange("p t j -> p j t"), 1.0, 0.0, op0=MULT, op1=ADD,
-            )
-        nc.vector.quantize_mx(out=c_codes[:].bitcast(FP8X4), scales=c_plane[:], in_=c_grouped[:])
+        quantise_c(1)
 
         three = {}
         for jt in FOLDED:
@@ -155,6 +168,10 @@ def tile_list_pnet_bias_kernel(
             nc.scalar.copy(out=own[:], in_=sums(TILES + jt, jt, with_own=True))
             three[jt] = keep.tile([P, P, PACK], BF16, name=f"three{jt}", align_bytes=64)
             nc.gpsimd.tensor_tensor(out=three[jt][:], in0=first[jt][:], in1=own[:], op=ADD)
+
+        for jt in ADDED:
+            round_c(jt)
+        quantise_c(0)
 
         pooled = {jt: rounded.tile([P, P, PACK], F32, name=f"pooled{jt}", align_bytes=64, offset=jt * 4 * R) for jt in ADDED}
         for g in (1, 2, 3):

@@ -1,6 +1,7 @@
 from contextlib import ExitStack
 
 import concourse.mybir as mybir
+from concourse.masks import make_identity
 
 K, R, N, T, J, G = 512, 512, 256, 4096, 512, 4
 FLOPS = 2 * K * R * J * (G + 1) + 2 * R * N * J
@@ -21,8 +22,9 @@ P = 128
 PACK = 4
 TILES = J // P
 FIRST_ROW = P - 16
-ADDED = (0, 1)
-FOLDED = (2, 3)
+FOLDED = (0, 1)
+TURNED = 2
+ADDED = 3
 
 
 def load_scale_rows(nc, plane, rows):
@@ -66,6 +68,8 @@ def tile_list_pnet_bias_kernel(
             for h in range(2)
         ]
 
+        identity = keep.tile([P, P], F32, name="identity", align_bytes=64)
+        make_identity(nc, identity[:])
         nc.vector.memset(zeros[:, : R // 4], 0)
         nc.vector.tensor_copy(w_plane[:].bitcast(I32), zeros[:, : R // 4])
         nc.vector.memset(tab_rows[:FIRST_ROW, :].bitcast(I32), 0)
@@ -85,7 +89,7 @@ def tile_list_pnet_bias_kernel(
             nc.sync.dma_start(out=picked_plane[r:P:32, :].bitcast(I32), in_=picked_rows[FIRST_ROW + r : P : 4, :].bitcast(I32))
         nc.gpsimd.memset(wd_plane[:].bitcast(I32), 0)
         c_rows = c.rearrange("(p t) j -> p t j", t=PACK)
-        for h in (1, 0):
+        for h in range(2):
             nc.sync.dma_start(out=c_raw[h][:], in_=c_rows[:, :, columns(h, J // 2)])
         nc.sync.dma_start(out=wd_codes[:].bitcast(I32), in_=wd_words[0].bitcast(I32))
         load_scale_rows(nc, wd_plane, wd_scales[0])
@@ -94,10 +98,12 @@ def tile_list_pnet_bias_kernel(
 
         w_dealt = keep.tile([P, R], I32, name="w_dealt", align_bytes=64)
         w_dealt_plane = keep.tile([P, R], U8, name="w_dealt_plane", align_bytes=64)
-        for dealt, source in ((w_dealt, w_codes), (w_dealt_plane, w_plane)):
-            nc.vector.tensor_copy(dealt[:].rearrange("p (t m) -> p t m", t=PACK), source[:].rearrange("p (m t) -> p t m", t=PACK))
+        nc.vector.tensor_copy(
+            w_dealt[:].rearrange("p (t m i) -> p m t i", t=PACK, i=4), w_codes[:].rearrange("p (m i t) -> p m t i", t=PACK, i=4)
+        )
+        nc.vector.tensor_copy(w_dealt_plane[:].rearrange("p (t m) -> p t m", t=PACK), w_plane[:].rearrange("p (m t) -> p t m", t=PACK))
 
-        picked_first = rounded.tile([P, J], U32, name="picked_first", align_bytes=64, offset=2 * R)
+        picked_first = rounded.tile([P, J], U32, name="picked_first", align_bytes=64, offset=0)
         picked_rest = dealt_from.tile([P, (G - 1) * J], U32, name="picked_rest", align_bytes=64, offset=0)
         picked = [picked_first[:]] + [picked_rest[:, columns(g, J)] for g in range(G - 1)]
         for g in range(G):
@@ -119,6 +125,13 @@ def tile_list_pnet_bias_kernel(
                 passes.append((w_dealt, w_dealt_plane, picked[g][:, columns(jt)], picked_plane[:, columns(g * TILES + jt)]))
             if with_own:
                 passes.append((wc_codes, wc_plane, c_codes[:, columns(jt)], c_plane[:, columns(jt)]))
+            if jt == TURNED:
+                moving, moving_plane, codes, plane = passes[0]
+                nc.tensor.matmul_mx(
+                    out=bank[:].rearrange("p t m -> p (t m)"), lhsT=codes.bitcast(FP8X4), lhsT_scale=plane,
+                    rhs=moving[:].bitcast(FP8X4), rhs_scale=moving_plane[:], start=True, stop=True,
+                )
+                return bank[:]
             for n, (codes, plane, moving, moving_plane) in enumerate(passes):
                 for t in range(PACK):
                     nc.tensor.matmul_mx(
@@ -128,68 +141,76 @@ def tile_list_pnet_bias_kernel(
                     )
             return bank[:].rearrange("p t j -> p j t")
 
-        first = {jt: keep.tile([P, P, PACK], F32, name=f"first{jt}", align_bytes=64) for jt in range(TILES)}
-        first_sums = {jt: sums(jt, jt, g=0) for jt in FOLDED + ADDED}
-        c_grouped = [
-            keep.tile([P, PACK * J // 2], BF16, name="c_grouped0", align_bytes=64),
-            rounded.tile([P, PACK * J // 2], BF16, name="c_grouped1", align_bytes=64, offset=2 * R),
-        ]
+        def layout(jt):
+            return [P, PACK, P] if jt == TURNED else [P, P, PACK]
 
-        def round_c(jt):
-            nc.scalar.copy(
-                out=c_grouped[jt // 2][:, columns(jt % 2, PACK * P)].rearrange("p (j i t) -> p j t i", i=4, t=PACK),
-                in_=c_raw[jt // 2][:, :, columns(jt % 2)].rearrange("p t (j i) -> p j t i", i=4),
-            )
-
-        def quantise_c(half):
-            cols = columns(half, J // 2)
-            nc.vector.quantize_mx(out=c_codes[:, cols].bitcast(FP8X4), scales=c_plane[:, cols], in_=c_grouped[half][:])
-
+        first = {jt: keep.tile(layout(jt), F32, name=f"first{jt}", align_bytes=64) for jt in range(TILES)}
+        first_sums = {jt: sums(jt, jt, g=0) for jt in FOLDED + (TURNED, ADDED)}
+        c_grouped = rounded.tile([P, 3 * 2 * R], BF16, name="c_grouped", align_bytes=64, offset=0)
         for jt in FOLDED:
             nc.scalar.copy(out=first[jt][:], in_=first_sums[jt])
-        for jt in FOLDED:
-            round_c(jt)
-        for jt in ADDED:
+        for half in range(2):
+            nc.scalar.copy(
+                out=c_grouped[:, columns(half, PACK * J // 2)].rearrange("p (j i t) -> p j t i", i=4, t=PACK),
+                in_=c_raw[half][:].rearrange("p t (j i) -> p j t i", i=4),
+            )
+        for jt in (TURNED, ADDED):
             nc.scalar.copy(out=first[jt][:], in_=first_sums[jt])
         nc.vector.quantize_mx(out=wc_codes[:].bitcast(FP8X4), scales=wc_plane[:], in_=wc_grouped[:])
 
         def maximum(target, earlier, g, jt):
             nc.vector.tensor_tensor(out=target[:], in0=sums((g % 2) * TILES + jt, jt, g=g), in1=earlier[:], op=MAX)
 
-        for g in (1, 2):
-            for jt in FOLDED:
-                maximum(first[jt], first[jt], g, jt)
-
-        quantise_c(1)
-
-        three = {}
-        for jt in FOLDED:
-            own = keep.tile([P, P, PACK], F32, name=f"own{jt}", align_bytes=64)
-            nc.scalar.copy(out=own[:], in_=sums(TILES + jt, jt, with_own=True))
-            three[jt] = keep.tile([P, P, PACK], BF16, name=f"three{jt}", align_bytes=64)
-            nc.gpsimd.tensor_tensor(out=three[jt][:], in0=first[jt][:], in1=own[:], op=ADD)
-
-        for jt in ADDED:
-            round_c(jt)
-        quantise_c(0)
-
-        pooled = {jt: rounded.tile([P, P, PACK], F32, name=f"pooled{jt}", align_bytes=64, offset=jt * 4 * R) for jt in ADDED}
-        for g in (1, 2, 3):
-            for jt in ADDED:
-                maximum(pooled[jt], first[jt] if g == 1 else pooled[jt], g, jt)
+        maximum(first[0], first[0], 1, 0)
+        maximum(first[1], first[1], 1, 1)
+        maximum(first[0], first[0], 2, 0)
+        nc.vector.quantize_mx(out=c_codes[:].bitcast(FP8X4), scales=c_plane[:], in_=c_grouped[:, : PACK * J])
+        pooled = {0: first[0]}
+        for slot, jt in enumerate((TURNED, ADDED, 1)):
+            pooled[jt] = rounded.tile(layout(jt), F32, name=f"pooled{jt}", align_bytes=64, offset=slot * 4 * R)
+        maximum(pooled[1], first[1], 2, 1)
 
         h_grouped = keep.tile([P, TILES, P, PACK], BF16, name="h_grouped", align_bytes=64)
         h_codes = keep.tile([P, J], U32, name="h_codes", align_bytes=64)
         h_plane = keep.tile([P, J], U8, name="h_plane", align_bytes=64)
-        for jt in ADDED:
-            signed = keep.tile([P, P, PACK], BF16, name=f"signed{jt}", align_bytes=64)
-            nc.vector.tensor_tensor(out=signed[:], in0=sums(FOLDED[jt], jt, with_own=True), in1=pooled[jt][:], op=ADD)
-            nc.scalar.activation(out=h_grouped[:, jt], in_=signed[:], func=ACT.Relu)
+        three = {}
+        last = {}
+        for jt in FOLDED:
+            own = keep.tile(layout(jt), F32, name=f"own{jt}", align_bytes=64)
+            nc.scalar.copy(out=own[:], in_=sums(jt, jt, with_own=True))
+            three[jt] = keep.tile(layout(jt), BF16, name=f"three{jt}", align_bytes=64)
+            nc.gpsimd.tensor_tensor(out=three[jt][:], in0=pooled[jt][:], in1=own[:], op=ADD)
+        folded = {jt: sums(TILES + jt, jt, g=3, with_own=True) for jt in FOLDED}
+
+        def round_folded(jt):
+            last[jt] = keep.tile(layout(jt), BF16, name=f"last{jt}", align_bytes=64)
+            nc.scalar.activation(out=last[jt][:], in_=folded[jt], func=ACT.Relu)
 
         def last_maximum(jt):
-            nc.vector.scalar_tensor_tensor(
-                out=h_grouped[:, jt], in0=sums(TILES + jt, jt, g=3, with_own=True), scalar=0.0, in1=three[jt][:], op0=MAX, op1=MAX,
-            )
+            nc.vector.tensor_tensor(out=h_grouped[:, jt], in0=last[jt][:], in1=three[jt][:], op=MAX)
+
+        round_folded(0)
+        own = keep.tile(layout(TURNED), F32, name="own_turned", align_bytes=64)
+        nc.scalar.copy(out=own[:], in_=sums(0, TURNED, with_own=True))
+        summed = psum.tile([P, PACK, P], F32, name="bank", tag="bank0")
+        for t in range(PACK):
+            nc.tensor.matmul(summed[:, t, :], own[:, t, :], identity[:], start=t == 0, stop=False, is_transpose=True)
+        round_folded(1)
+
+        for g in (1, 2):
+            for jt in (TURNED, ADDED):
+                maximum(pooled[jt], first[jt] if g == 1 else pooled[jt], g, jt)
+        maximum(pooled[TURNED], pooled[TURNED], 3, TURNED)
+        for t in range(PACK):
+            nc.tensor.matmul(summed[:, t, :], pooled[TURNED][:, t, :], identity[:], start=False, stop=t == PACK - 1, is_transpose=True)
+        nc.scalar.activation(out=h_grouped[:, TURNED], in_=summed[:].rearrange("p t j -> p j t"), func=ACT.Relu)
+        own_sums = sums(1, ADDED, with_own=True)
+        maximum(pooled[ADDED], pooled[ADDED], 3, ADDED)
+        last_maximum(0)
+        signed = keep.tile(layout(ADDED), BF16, name="signed", align_bytes=64)
+        nc.vector.tensor_tensor(out=signed[:], in0=own_sums, in1=pooled[ADDED][:], op=ADD)
+        nc.scalar.activation(out=h_grouped[:, ADDED], in_=signed[:], func=ACT.Relu)
+        last_maximum(1)
 
         def quantise(first_tile, count):
             cols = slice(first_tile * P, (first_tile + count) * P)
@@ -206,22 +227,24 @@ def tile_list_pnet_bias_kernel(
         def add_bias_vector(result, y, h):
             nc.vector.tensor_scalar(result, y, bias[:, h : h + 1], None, op0=ADD)
 
-        def finish(pair, banks, adders, queues):
-            cols = columns(pair, 2 * P)
-            for h in range(2):
-                y = psum.tile([P, 2 * P], F32, name="bank", tag=f"bank{banks[h]}")
+        results = [keep.tile([P, J], F32, name=f"result{h}", align_bytes=64) for h in range(2)]
+
+        def finish(first_tile, count, banks):
+            cols = slice(first_tile * P, (first_tile + count) * P)
+            for h, add_bias in enumerate((add_bias_scalar, add_bias_vector)):
+                y = psum.tile([P, count * P], F32, name="bank", tag=f"bank{banks[h]}")
                 nc.tensor.matmul_mx(
                     out=y[:], lhsT=wd_codes[:, columns(h, 2 * P)].bitcast(FP4X4), lhsT_scale=wd_plane[:, columns(h)],
                     rhs=h_codes[:, cols].bitcast(FP8X4), rhs_scale=h_plane[:, cols], start=True, stop=True,
                 )
-                result = keep.tile([P, 2 * P], F32, name=f"result{pair}{h}")
-                adders[h](result[:], y[:], h)
-                queues[h].dma_start(out=out_rows[:, h, cols], in_=result[:])
+                add_bias(results[h][:, cols], y[:], h)
 
-        last_maximum(2)
-        quantise(0, 2)
-        last_maximum(3)
-        quantise(2, 1)
-        quantise(3, 1)
-        finish(0, (0, 1), (add_bias_scalar, add_bias_scalar), (nc.sync, nc.sync))
-        finish(1, (4, 5), (add_bias_scalar, add_bias_vector), (nc.scalar, nc.sync))
+        for jt in range(TILES):
+            quantise(jt, 1)
+        finish(0, 2, (2, 3))
+        finish(TURNED, 1, (6, 7))
+        for h in range(2):
+            nc.sync.dma_start(out=out_rows[:, h, : ADDED * P], in_=results[h][:, : ADDED * P])
+        finish(ADDED, 1, (4, 5))
+        for h, queue in enumerate((nc.scalar, nc.sync)):
+            queue.dma_start(out=out_rows[:, h, ADDED * P :], in_=results[h][:, ADDED * P :])

@@ -57,7 +57,6 @@ def tile_list_pnet_bias_kernel(
         tab_rows = loads.tile([P, T], U8, name="tab_rows", align_bytes=64, offset=4 * PACK * (R + J // 4))
         between = 4 * PACK * (R + J // 2)
         wd_codes = loads.tile([P, 2 * N], U8, name="wd_codes", align_bytes=64, offset=between)
-        wd_plane = loads.tile([P, N], U8, name="wd_plane", align_bytes=64, offset=between + 2 * N)
         bias = loads.tile([P, N // P], F32, name="bias", align_bytes=64, offset=between + 3 * N)
         wc_raw = [
             loads.tile([P, PACK, R // 2], F32, name=f"wc_raw{h}", align_bytes=64, offset=4 * h * PACK * R // 2)
@@ -70,9 +69,9 @@ def tile_list_pnet_bias_kernel(
 
         identity = keep.tile([P, P], F32, name="identity", align_bytes=64)
         make_identity(nc, identity[:])
+        nc.vector.memset(tab_rows[:FIRST_ROW, :].bitcast(I32), 0)
         nc.vector.memset(zeros[:, : R // 4], 0)
         nc.vector.tensor_copy(w_plane[:].bitcast(I32), zeros[:, : R // 4])
-        nc.vector.memset(tab_rows[:FIRST_ROW, :].bitcast(I32), 0)
         nc.vector.memset(picked_plane[:].bitcast(I32), 0)
 
         nc.sync.dma_start(offsets[:], offs)
@@ -87,12 +86,10 @@ def tile_list_pnet_bias_kernel(
         nc.vector.tensor_copy(picked_rows[:], tab_rows[:].indirect(offsets[:]))
         for r in range(4):
             nc.sync.dma_start(out=picked_plane[r:P:32, :].bitcast(I32), in_=picked_rows[FIRST_ROW + r : P : 4, :].bitcast(I32))
-        nc.gpsimd.memset(wd_plane[:].bitcast(I32), 0)
         c_rows = c.rearrange("(p t) j -> p t j", t=PACK)
         for h in range(2):
             nc.sync.dma_start(out=c_raw[h][:], in_=c_rows[:, :, columns(h, J // 2)])
         nc.sync.dma_start(out=wd_codes[:].bitcast(I32), in_=wd_words[0].bitcast(I32))
-        load_scale_rows(nc, wd_plane, wd_scales[0])
         with nc.allow_non_contiguous_dma(reason="one bias value a partition"):
             nc.sync.dma_start(out=bias[:], in_=b.rearrange("(h p) -> p h", p=P))
 
@@ -109,7 +106,7 @@ def tile_list_pnet_bias_kernel(
         for g in range(G):
             nc.vector.tensor_copy(picked[g], table[:].bitcast(U32).indirect(offsets[:, columns(g, J // 16)]))
 
-        wc_grouped = keep.tile([P, PACK * R], BF16, name="wc_grouped", align_bytes=64)
+        wc_grouped = rounded.tile([P, PACK * R], BF16, name="wc_grouped", align_bytes=64, offset=16 * R)
         wc_codes = keep.tile([P, R], U32, name="wc_codes", align_bytes=64)
         wc_plane = keep.tile([P, R], U8, name="wc_plane", align_bytes=64)
         c_codes = keep.tile([P, J], U32, name="c_codes", align_bytes=64)
@@ -157,9 +154,12 @@ def tile_list_pnet_bias_kernel(
         for jt in (TURNED, ADDED):
             nc.scalar.copy(out=first[jt][:], in_=first_sums[jt])
         nc.vector.quantize_mx(out=wc_codes[:].bitcast(FP8X4), scales=wc_plane[:], in_=wc_grouped[:])
+        wd_plane = rounded.tile([P, N], U8, name="wd_plane", align_bytes=64, offset=16 * R)
+        nc.gpsimd.memset(wd_plane[:].bitcast(I32), 0)
+        load_scale_rows(nc, wd_plane, wd_scales[0])
 
         def maximum(target, earlier, g, jt):
-            nc.vector.tensor_tensor(out=target[:], in0=sums((g % 2) * TILES + jt, jt, g=g), in1=earlier[:], op=MAX)
+            nc.vector.tensor_tensor(out=target[:], in0=earlier[:], in1=sums((g % 2) * TILES + jt, jt, g=g), op=MAX)
 
         maximum(first[0], first[0], 1, 0)
         maximum(first[1], first[1], 1, 1)
@@ -208,7 +208,7 @@ def tile_list_pnet_bias_kernel(
         maximum(pooled[ADDED], pooled[ADDED], 3, ADDED)
         last_maximum(0)
         signed = keep.tile(layout(ADDED), BF16, name="signed", align_bytes=64)
-        nc.vector.tensor_tensor(out=signed[:], in0=own_sums, in1=pooled[ADDED][:], op=ADD)
+        nc.vector.tensor_tensor(out=signed[:], in0=pooled[ADDED][:], in1=own_sums, op=ADD)
         nc.scalar.activation(out=h_grouped[:, ADDED], in_=signed[:], func=ACT.Relu)
         last_maximum(1)
 

@@ -74,8 +74,8 @@ def tile_list_pnet_bias_kernel(
         nc.vector.tensor_copy(w_plane[:].bitcast(I32), zeros[:, : R // 4])
         nc.vector.memset(picked_plane[:].bitcast(I32), 0)
 
-        nc.sync.dma_start(offsets[:], offs)
         nc.sync.dma_start(out=tab_rows[FIRST_ROW:, :].bitcast(I32), in_=tab_scales[0].bitcast(I32))
+        nc.sync.dma_start(offsets[:], offs)
         nc.sync.dma_start(out=table[:], in_=tab_words[0].rearrange("p t i -> p (t i)").bitcast(I32))
         nc.sync.dma_start(out=w_codes[:], in_=w_words[0].rearrange("p r i -> p (r i)").bitcast(I32))
         load_scale_rows(nc, w_plane, w_scales[0])
@@ -239,12 +239,13 @@ def tile_list_pnet_bias_kernel(
                 )
                 add_bias(results[h][:, cols], y[:], h)
 
-        for jt in range(TILES):
-            quantise(jt, 1)
+        quantise(0, 1)
+        quantise(TURNED, 1)
+        quantise(1, 1)
+        quantise(ADDED, 1)
         finish(0, 2, (2, 3))
-        finish(TURNED, 1, (6, 7))
         for h in range(2):
-            nc.sync.dma_start(out=out_rows[:, h, : ADDED * P], in_=results[h][:, : ADDED * P])
-        finish(ADDED, 1, (4, 5))
+            nc.sync.dma_start(out=out_rows[:, h, : J // 2], in_=results[h][:, : J // 2])
+        finish(2, 2, (6, 7))
         for h, queue in enumerate((nc.scalar, nc.sync)):
-            queue.dma_start(out=out_rows[:, h, ADDED * P :], in_=results[h][:, ADDED * P :])
+            queue.dma_start(out=out_rows[:, h, J // 2 :], in_=results[h][:, J // 2 :])

@@ -17,23 +17,25 @@ FP4X4 = mybir.dt.float4_e2m1fn_x4
 ACT = mybir.ActivationFunctionType
 MAX = mybir.AluOpType.max
 ADD = mybir.AluOpType.add
+MULT = mybir.AluOpType.mult
 
 P = 128
 PACK = 4
 TILES = J // P
 FIRST_ROW = P - 16
 FOLDED = (0, 1)
-TURNED = 2
-ADDED = 3
-
-
-def load_scale_rows(nc, plane, rows):
-    for r in range(4):
-        nc.sync.dma_start(out=plane[r:P:32, :].bitcast(I32), in_=rows[r:16:4, :].bitcast(I32))
+TURNED = (2, 3)
+HALF = 4 * PACK * J // 2
+PAD = HALF // 4
 
 
 def columns(tile, width=P):
     return slice(tile * width, (tile + 1) * width)
+
+
+def move_home(nc, plane, rows):
+    for r in range(4):
+        nc.sync.dma_start(out=plane[r:P:32, :].bitcast(I32), in_=rows[FIRST_ROW + r : P : 4, :].bitcast(I32))
 
 
 def tile_list_pnet_bias_kernel(
@@ -42,50 +44,49 @@ def tile_list_pnet_bias_kernel(
     nc = tc.nc
     with ExitStack() as ctx:
         keep = ctx.enter_context(tc.tile_pool(name="keep", bufs=1))
-        loads = ctx.enter_context(tc.tile_pool(name="loads", bufs=1))
+        wc_side = ctx.enter_context(tc.tile_pool(name="wc_side", bufs=1))
+        c_side = ctx.enter_context(tc.tile_pool(name="c_side", bufs=1))
         rounded = ctx.enter_context(tc.tile_pool(name="rounded", bufs=1))
-        dealt_from = ctx.enter_context(tc.tile_pool(name="dealt_from", bufs=1))
+        ending = ctx.enter_context(tc.tile_pool(name="ending", bufs=1))
         psum = ctx.enter_context(tc.psum_pool(name="psum", bufs=1))
 
         offsets = keep.tile([P, G * J // 16], U16, name="offsets")
         picked_rows = keep.tile([P, G * J], U8, name="picked_rows", align_bytes=64)
         picked_plane = keep.tile([P, G * J], U8, name="picked_plane", align_bytes=64)
-        w_plane = dealt_from.tile([P, R], U8, name="w_plane", align_bytes=64, offset=4 * R)
         table = keep.tile([P, T], I32, name="table", align_bytes=64)
-        w_codes = dealt_from.tile([P, R], I32, name="w_codes", align_bytes=64, offset=0)
-        zeros = loads.tile([P, PACK * R], I32, name="zeros", align_bytes=64, offset=0)
-        tab_rows = loads.tile([P, T], U8, name="tab_rows", align_bytes=64, offset=4 * PACK * (R + J // 4))
-        between = 4 * PACK * (R + J // 2)
-        wd_codes = loads.tile([P, 2 * N], U8, name="wd_codes", align_bytes=64, offset=between)
-        bias = loads.tile([P, N // P], F32, name="bias", align_bytes=64, offset=between + 3 * N)
-        wc_raw = [
-            loads.tile([P, PACK, R // 2], F32, name=f"wc_raw{h}", align_bytes=64, offset=4 * h * PACK * R // 2)
-            for h in range(2)
-        ]
-        c_raw = [
-            loads.tile([P, PACK, J // 2], F32, name=f"c_raw{h}", align_bytes=64, offset=4 * PACK * R + h * (4 * PACK * J // 2 + 4 * N))
-            for h in range(2)
-        ]
+        w_codes = keep.tile([P, R], I32, name="w_codes", align_bytes=64)
+        weight_rows = keep.tile([P, R + N], U8, name="weight_rows", align_bytes=64)
+        weight_plane = keep.tile([P, R + N], U8, name="weight_plane", align_bytes=64)
+        w_rows = wc_side.tile([P, R], U8, name="w_rows", align_bytes=64, offset=HALF - R // 2)
+        wc_raw = [wc_side.tile([P, PACK, R // 2], F32, name=f"wc_raw{h}", align_bytes=64, offset=h * HALF) for h in range(2)]
+        tab_rows = c_side.tile([P, T], U8, name="tab_rows", align_bytes=64, offset=HALF - PAD)
+        wd_codes = c_side.tile([P, 2 * N], U8, name="wd_codes", align_bytes=64, offset=HALF)
+        bias = c_side.tile([P, N // P], F32, name="bias", align_bytes=64, offset=HALF + 3 * N)
+        c_start = [HALF + 2 * PAD, 0]
+        c_raw = [c_side.tile([P, PACK, J // 2], F32, name=f"c_raw{h}", align_bytes=64, offset=c_start[h]) for h in range(2)]
 
         identity = keep.tile([P, P], F32, name="identity", align_bytes=64)
         make_identity(nc, identity[:])
+        nc.vector.memset(w_rows[:FIRST_ROW, :].bitcast(I32), 0)
         nc.vector.memset(tab_rows[:FIRST_ROW, :].bitcast(I32), 0)
-        nc.vector.memset(zeros[:, : R // 4], 0)
-        nc.vector.tensor_copy(w_plane[:].bitcast(I32), zeros[:, : R // 4])
+        nc.vector.memset(weight_plane[:].bitcast(I32), 0)
         nc.vector.memset(picked_plane[:].bitcast(I32), 0)
 
+        nc.scalar.dma_start(out=weight_rows[FIRST_ROW:, R:].bitcast(I32), in_=wd_scales[0].bitcast(I32))
+        nc.scalar.dma_start(out=w_rows[FIRST_ROW:, :].bitcast(I32), in_=w_scales[0].bitcast(I32))
         nc.sync.dma_start(out=tab_rows[FIRST_ROW:, :].bitcast(I32), in_=tab_scales[0].bitcast(I32))
         nc.sync.dma_start(offsets[:], offs)
-        nc.sync.dma_start(out=table[:], in_=tab_words[0].rearrange("p t i -> p (t i)").bitcast(I32))
         nc.sync.dma_start(out=w_codes[:], in_=w_words[0].rearrange("p r i -> p (r i)").bitcast(I32))
-        load_scale_rows(nc, w_plane, w_scales[0])
+        nc.sync.dma_start(out=table[:], in_=tab_words[0].rearrange("p t i -> p (t i)").bitcast(I32))
+
+        nc.vector.tensor_copy(weight_rows[:, :R].rearrange("p (t m) -> p t m", t=PACK), w_rows[:].rearrange("p (m t) -> p t m", t=PACK))
+        move_home(nc, weight_plane, weight_rows)
         wc_rows = wc.rearrange("(p t) r -> p t r", t=PACK)
         for h in range(2):
             nc.sync.dma_start(out=wc_raw[h][:], in_=wc_rows[:, :, columns(h, R // 2)])
 
         nc.vector.tensor_copy(picked_rows[:], tab_rows[:].indirect(offsets[:]))
-        for r in range(4):
-            nc.sync.dma_start(out=picked_plane[r:P:32, :].bitcast(I32), in_=picked_rows[FIRST_ROW + r : P : 4, :].bitcast(I32))
+        move_home(nc, picked_plane, picked_rows)
         c_rows = c.rearrange("(p t) j -> p t j", t=PACK)
         for h in range(2):
             nc.sync.dma_start(out=c_raw[h][:], in_=c_rows[:, :, columns(h, J // 2)])
@@ -94,39 +95,33 @@ def tile_list_pnet_bias_kernel(
             nc.sync.dma_start(out=bias[:], in_=b.rearrange("(h p) -> p h", p=P))
 
         w_dealt = keep.tile([P, R], I32, name="w_dealt", align_bytes=64)
-        w_dealt_plane = keep.tile([P, R], U8, name="w_dealt_plane", align_bytes=64)
         nc.vector.tensor_copy(
             w_dealt[:].rearrange("p (t m i) -> p m t i", t=PACK, i=4), w_codes[:].rearrange("p (m i t) -> p m t i", t=PACK, i=4)
         )
-        nc.vector.tensor_copy(w_dealt_plane[:].rearrange("p (t m) -> p t m", t=PACK), w_plane[:].rearrange("p (m t) -> p t m", t=PACK))
+        picked_pairs = [keep.tile([P, 2 * J], U32, name=f"picked{n}", align_bytes=64) for n in range(2)]
+        for n in range(2):
+            nc.vector.tensor_copy(picked_pairs[n][:], table[:].bitcast(U32).indirect(offsets[:, columns(n, 2 * J // 16)]))
+        picked = [picked_pairs[g // 2][:, columns(g % 2, J)] for g in range(G)]
 
-        picked_first = rounded.tile([P, J], U32, name="picked_first", align_bytes=64, offset=0)
-        picked_rest = dealt_from.tile([P, (G - 1) * J], U32, name="picked_rest", align_bytes=64, offset=0)
-        picked = [picked_first[:]] + [picked_rest[:, columns(g, J)] for g in range(G - 1)]
-        for g in range(G):
-            nc.vector.tensor_copy(picked[g], table[:].bitcast(U32).indirect(offsets[:, columns(g, J // 16)]))
-
-        wc_grouped = rounded.tile([P, PACK * R], BF16, name="wc_grouped", align_bytes=64, offset=16 * R)
+        wc_grouped = keep.tile([P, PACK * R], BF16, name="wc_grouped", align_bytes=64)
         wc_codes = keep.tile([P, R], U32, name="wc_codes", align_bytes=64)
         wc_plane = keep.tile([P, R], U8, name="wc_plane", align_bytes=64)
-        c_codes = keep.tile([P, J], U32, name="c_codes", align_bytes=64)
-        c_plane = keep.tile([P, J], U8, name="c_plane", align_bytes=64)
-        wc_dealt = wc_grouped[:].rearrange("p (t h m i) -> p h m i t", t=PACK, h=2, i=PACK)
-        for h in range(2):
-            nc.scalar.copy(out=wc_dealt[:, h], in_=wc_raw[h][:].rearrange("p i (m t) -> p m i t", t=PACK))
+        c_grouped = [rounded.tile([P, PACK * J // 2], BF16, name=f"c_grouped{h}", align_bytes=64, offset=0) for h in range(2)]
+        c_codes = [keep.tile([P, J // 2], U32, name=f"c_codes{h}", align_bytes=64) for h in range(2)]
+        c_plane = [keep.tile([P, J // 2], U8, name=f"c_plane{h}", align_bytes=64) for h in range(2)]
 
         def sums(index, jt, g=None, with_own=False):
             bank = psum.tile([P, PACK, P], F32, name="bank", tag=f"bank{index}")
             passes = []
             if g is not None:
-                passes.append((w_dealt, w_dealt_plane, picked[g][:, columns(jt)], picked_plane[:, columns(g * TILES + jt)]))
+                passes.append((w_dealt[:], weight_plane[:, :R], picked[g][:, columns(jt)], picked_plane[:, columns(g * TILES + jt)]))
             if with_own:
-                passes.append((wc_codes, wc_plane, c_codes[:, columns(jt)], c_plane[:, columns(jt)]))
-            if jt == TURNED:
+                passes.append((wc_codes[:], wc_plane[:], c_codes[jt // 2][:, columns(jt % 2)], c_plane[jt // 2][:, columns(jt % 2)]))
+            if jt in TURNED:
                 moving, moving_plane, codes, plane = passes[0]
                 nc.tensor.matmul_mx(
                     out=bank[:].rearrange("p t m -> p (t m)"), lhsT=codes.bitcast(FP8X4), lhsT_scale=plane,
-                    rhs=moving[:].bitcast(FP8X4), rhs_scale=moving_plane[:], start=True, stop=True,
+                    rhs=moving.bitcast(FP8X4), rhs_scale=moving_plane, start=True, stop=True,
                 )
                 return bank[:]
             for n, (codes, plane, moving, moving_plane) in enumerate(passes):
@@ -139,85 +134,107 @@ def tile_list_pnet_bias_kernel(
             return bank[:].rearrange("p t j -> p j t")
 
         def layout(jt):
-            return [P, PACK, P] if jt == TURNED else [P, P, PACK]
+            return [P, PACK, P] if jt in TURNED else [P, P, PACK]
 
-        first = {jt: keep.tile(layout(jt), F32, name=f"first{jt}", align_bytes=64) for jt in range(TILES)}
-        first_sums = {jt: sums(jt, jt, g=0) for jt in FOLDED + (TURNED, ADDED)}
-        c_grouped = rounded.tile([P, 3 * 2 * R], BF16, name="c_grouped", align_bytes=64, offset=0)
-        for jt in FOLDED:
-            nc.scalar.copy(out=first[jt][:], in_=first_sums[jt])
-        for half in range(2):
+        def round_c(h):
             nc.scalar.copy(
-                out=c_grouped[:, columns(half, PACK * J // 2)].rearrange("p (j i t) -> p j t i", i=4, t=PACK),
-                in_=c_raw[half][:].rearrange("p t (j i) -> p j t i", i=4),
+                out=c_grouped[h][:].rearrange("p (j i t) -> p j t i", i=4, t=PACK),
+                in_=c_raw[h][:].rearrange("p t (j i) -> p j t i", i=4),
             )
-        for jt in (TURNED, ADDED):
-            nc.scalar.copy(out=first[jt][:], in_=first_sums[jt])
+
+        def quantise_c(h):
+            nc.vector.quantize_mx(out=c_codes[h][:].bitcast(FP8X4), scales=c_plane[h][:], in_=c_grouped[h][:])
+
+        pooled = {}
+
+        def first_copy(jt, bank):
+            if jt == 3:
+                pooled[jt] = keep.tile(layout(jt), F32, name="pooled3", align_bytes=64)
+            else:
+                start = c_start[0] - PAD + jt * HALF // 2
+                pooled[jt] = c_side.tile(layout(jt), F32, name=f"pooled{jt}", align_bytes=64, offset=start)
+            nc.scalar.copy(out=pooled[jt][:], in_=bank)
+
+        def maximum(jt, bank):
+            nc.vector.tensor_tensor(out=pooled[jt][:], in0=pooled[jt][:], in1=bank, op=MAX)
+
+        own = {}
+
+        def own_copy(jt, bank):
+            own[jt] = keep.tile(layout(jt), F32, name=f"own{jt}", align_bytes=64)
+            nc.scalar.copy(out=own[jt][:], in_=bank)
+
+        early = {(jt, g): sums(2 * g + jt, jt, g=g) for g in range(2) for jt in FOLDED}
+        early[2, 0] = sums(6, 2, g=0)
+        early[1, 2] = sums(4, 1, g=2)
+
+        wc_dealt = wc_grouped[:].rearrange("p (t h m i) -> p h m i t", t=PACK, h=2, i=PACK)
+        for h in range(2):
+            nc.scalar.copy(out=wc_dealt[:, h], in_=wc_raw[h][:].rearrange("p i (m t) -> p m i t", t=PACK))
         nc.vector.quantize_mx(out=wc_codes[:].bitcast(FP8X4), scales=wc_plane[:], in_=wc_grouped[:])
-        wd_plane = rounded.tile([P, N], U8, name="wd_plane", align_bytes=64, offset=16 * R)
-        nc.gpsimd.memset(wd_plane[:].bitcast(I32), 0)
-        load_scale_rows(nc, wd_plane, wd_scales[0])
-
-        def maximum(target, earlier, g, jt):
-            nc.vector.tensor_tensor(out=target[:], in0=earlier[:], in1=sums((g % 2) * TILES + jt, jt, g=g), op=MAX)
-
-        maximum(first[0], first[0], 1, 0)
-        maximum(first[1], first[1], 1, 1)
-        maximum(first[0], first[0], 2, 0)
-        nc.vector.quantize_mx(out=c_codes[:].bitcast(FP8X4), scales=c_plane[:], in_=c_grouped[:, : PACK * J])
-        pooled = {0: first[0]}
-        for slot, jt in enumerate((TURNED, ADDED, 1)):
-            pooled[jt] = rounded.tile(layout(jt), F32, name=f"pooled{jt}", align_bytes=64, offset=slot * 4 * R)
-        maximum(pooled[1], first[1], 2, 1)
-
-        h_grouped = keep.tile([P, TILES, P, PACK], BF16, name="h_grouped", align_bytes=64)
-        h_codes = keep.tile([P, J], U32, name="h_codes", align_bytes=64)
-        h_plane = keep.tile([P, J], U8, name="h_plane", align_bytes=64)
+        round_c(0)
+        quantise_c(0)
+        first_copy(0, early[0, 0])
+        early[3, 0] = sums(0, 3, g=0)
+        first_copy(1, early[1, 0])
+        maximum(0, early[0, 1])
+        nc.gpsimd.tensor_scalar(
+            c_grouped[1][:].rearrange("p (j t) -> p j t", t=PACK), c_raw[1][:].rearrange("p t j -> p j t"), 1.0, 0.0, op0=MULT, op1=ADD
+        )
+        own_banks = (7, 5)
+        own_sums = sums(own_banks[0], 0, with_own=True)
+        early[0, 2] = sums(1, 0, g=2)
+        maximum(1, early[1, 1])
+        for jt in TURNED:
+            first_copy(jt, early[jt, 0])
+        own_copy(0, own_sums)
+        own_copy(1, sums(own_banks[1], 1, with_own=True))
+        second = {jt: sums(jt, jt, g=1) for jt in TURNED}
+        for jt in FOLDED:
+            maximum(jt, early[jt, 2])
+        quantise_c(1)
         three = {}
+        for jt in FOLDED:
+            three[jt] = rounded.tile(layout(jt), BF16, name=f"three{jt}", align_bytes=64, offset=jt * HALF // 4)
+            nc.gpsimd.tensor_tensor(out=three[jt][:], in0=pooled[jt][:], in1=own[jt][:], op=ADD)
+        folded = {}
+        third = {}
+        for jt in TURNED:
+            third[jt] = sums((6, 0)[jt - 2], jt, g=2)
+            own_copy(jt, sums(own_banks[jt - 2], jt, with_own=True))
+        for jt in TURNED:
+            maximum(jt, second[jt])
+        fourth = {}
+        for jt in FOLDED:
+            folded[jt] = sums((1, 4)[jt], jt, g=3, with_own=True)
+            fourth[jt + 2] = sums(jt + 2, jt + 2, g=3)
         last = {}
         for jt in FOLDED:
-            own = keep.tile(layout(jt), F32, name=f"own{jt}", align_bytes=64)
-            nc.scalar.copy(out=own[:], in_=sums(jt, jt, with_own=True))
-            three[jt] = keep.tile(layout(jt), BF16, name=f"three{jt}", align_bytes=64)
-            nc.gpsimd.tensor_tensor(out=three[jt][:], in0=pooled[jt][:], in1=own[:], op=ADD)
-        folded = {jt: sums(TILES + jt, jt, g=3, with_own=True) for jt in FOLDED}
-
-        def round_folded(jt):
             last[jt] = keep.tile(layout(jt), BF16, name=f"last{jt}", align_bytes=64)
             nc.scalar.activation(out=last[jt][:], in_=folded[jt], func=ACT.Relu)
+        summed = {}
+        for jt in TURNED:
+            summed[jt] = psum.tile([P, PACK, P], F32, name="bank", tag=f"bank{own_banks[jt - 2]}")
+            for t in range(PACK):
+                nc.tensor.matmul(summed[jt][:, t, :], own[jt][:, t, :], identity[:], start=t == 0, stop=False, is_transpose=True)
+        for jt in TURNED:
+            maximum(jt, third[jt])
 
-        def last_maximum(jt):
-            nc.vector.tensor_tensor(out=h_grouped[:, jt], in0=last[jt][:], in1=three[jt][:], op=MAX)
-
-        round_folded(0)
-        own = keep.tile(layout(TURNED), F32, name="own_turned", align_bytes=64)
-        nc.scalar.copy(out=own[:], in_=sums(0, TURNED, with_own=True))
-        summed = psum.tile([P, PACK, P], F32, name="bank", tag="bank0")
-        for t in range(PACK):
-            nc.tensor.matmul(summed[:, t, :], own[:, t, :], identity[:], start=t == 0, stop=False, is_transpose=True)
-        round_folded(1)
-
-        for g in (1, 2):
-            for jt in (TURNED, ADDED):
-                maximum(pooled[jt], first[jt] if g == 1 else pooled[jt], g, jt)
-        maximum(pooled[TURNED], pooled[TURNED], 3, TURNED)
-        for t in range(PACK):
-            nc.tensor.matmul(summed[:, t, :], pooled[TURNED][:, t, :], identity[:], start=False, stop=t == PACK - 1, is_transpose=True)
-        nc.scalar.activation(out=h_grouped[:, TURNED], in_=summed[:].rearrange("p t j -> p j t"), func=ACT.Relu)
-        own_sums = sums(1, ADDED, with_own=True)
-        maximum(pooled[ADDED], pooled[ADDED], 3, ADDED)
-        last_maximum(0)
-        signed = keep.tile(layout(ADDED), BF16, name="signed", align_bytes=64)
-        nc.vector.tensor_tensor(out=signed[:], in0=pooled[ADDED][:], in1=own_sums, op=ADD)
-        nc.scalar.activation(out=h_grouped[:, ADDED], in_=signed[:], func=ACT.Relu)
-        last_maximum(1)
+        h_grouped = [ending.tile([P, 2, P, PACK], BF16, name=f"h_grouped{h}", align_bytes=64, offset=h * HALF // 2) for h in range(2)]
+        h_codes = keep.tile([P, J], U32, name="h_codes", align_bytes=64)
+        h_plane = keep.tile([P, J], U8, name="h_plane", align_bytes=64)
+        for jt in TURNED:
+            maximum(jt, fourth[jt])
+            for t in range(PACK):
+                nc.tensor.matmul(summed[jt][:, t, :], pooled[jt][:, t, :], identity[:], start=False, stop=t == PACK - 1, is_transpose=True)
+            nc.scalar.activation(out=h_grouped[1][:, jt - 2], in_=summed[jt][:].rearrange("p t j -> p j t"), func=ACT.Relu)
+        for jt in FOLDED:
+            nc.vector.tensor_tensor(out=h_grouped[0][:, jt], in0=last[jt][:], in1=three[jt][:], op=MAX)
 
         def quantise(first_tile, count):
             cols = slice(first_tile * P, (first_tile + count) * P)
-            nc.vector.quantize_mx(
-                out=h_codes[:, cols].bitcast(FP8X4), scales=h_plane[:, cols],
-                in_=h_grouped[:, first_tile : first_tile + count].rearrange("p a j t -> p (a j t)"),
-            )
+            source = h_grouped[first_tile // 2][:, first_tile % 2 : first_tile % 2 + count]
+            nc.vector.quantize_mx(out=h_codes[:, cols].bitcast(FP8X4), scales=h_plane[:, cols], in_=source.rearrange("p a j t -> p (a j t)"))
 
         out_rows = out.rearrange("(h p) j -> p h j", p=P)
 
@@ -227,25 +244,28 @@ def tile_list_pnet_bias_kernel(
         def add_bias_vector(result, y, h):
             nc.vector.tensor_scalar(result, y, bias[:, h : h + 1], None, op0=ADD)
 
-        results = [keep.tile([P, J], F32, name=f"result{h}", align_bytes=64) for h in range(2)]
+        results = {(h, pair): keep.tile([P, J // 2], F32, name=f"result{h}{pair}", align_bytes=64) for h, pair in ((0, 0), (0, 1), (1, 1))}
+        results[1, 0] = ending.tile([P, J // 2], F32, name="result10", align_bytes=64, offset=HALF // 2)
 
-        def finish(first_tile, count, banks):
-            cols = slice(first_tile * P, (first_tile + count) * P)
+        def finish(first_tile, width, banks):
+            y = [psum.tile([P, 2 * P], F32, name="bank", tag=f"bank{banks[h]}") for h in range(2)]
+            for start in range(0, 2 * P, width):
+                cols = slice(first_tile * P + start, first_tile * P + start + width)
+                for h in range(2):
+                    nc.tensor.matmul_mx(
+                        out=y[h][:, start : start + width], lhsT=wd_codes[:, columns(h, 2 * P)].bitcast(FP4X4),
+                        lhsT_scale=weight_plane[:, R + h * P : R + (h + 1) * P],
+                        rhs=h_codes[:, cols].bitcast(FP8X4), rhs_scale=h_plane[:, cols], start=True, stop=True,
+                    )
             for h, add_bias in enumerate((add_bias_scalar, add_bias_vector)):
-                y = psum.tile([P, count * P], F32, name="bank", tag=f"bank{banks[h]}")
-                nc.tensor.matmul_mx(
-                    out=y[:], lhsT=wd_codes[:, columns(h, 2 * P)].bitcast(FP4X4), lhsT_scale=wd_plane[:, columns(h)],
-                    rhs=h_codes[:, cols].bitcast(FP8X4), rhs_scale=h_plane[:, cols], start=True, stop=True,
-                )
-                add_bias(results[h][:, cols], y[:], h)
+                add_bias(results[h, first_tile // 2][:], y[h][:], h)
 
-        quantise(0, 1)
-        quantise(TURNED, 1)
-        quantise(1, 1)
-        quantise(ADDED, 1)
-        finish(0, 2, (2, 3))
+        quantise(0, 2)
+        quantise(2, 1)
+        quantise(3, 1)
+        finish(0, 2 * P, (1, 4))
         for h in range(2):
-            nc.sync.dma_start(out=out_rows[:, h, : J // 2], in_=results[h][:, : J // 2])
-        finish(2, 2, (6, 7))
+            nc.sync.dma_start(out=out_rows[:, h, : J // 2], in_=results[h, 0][:])
+        finish(2, P, (6, 0))
         for h, queue in enumerate((nc.scalar, nc.sync)):
-            queue.dma_start(out=out_rows[:, h, J // 2 :], in_=results[h][:, J // 2 :])
+            queue.dma_start(out=out_rows[:, h, J // 2 :], in_=results[h, 1][:])

@@ -148,7 +148,9 @@ def tile_list_pnet_bias_kernel(
         pooled = {}
 
         def first_copy(jt, bank):
-            if jt == 3:
+            if jt == 0:
+                pooled[jt] = wc_side.tile(layout(jt), F32, name="pooled0", align_bytes=64, offset=HALF)
+            elif jt == 3:
                 pooled[jt] = keep.tile(layout(jt), F32, name="pooled3", align_bytes=64)
             else:
                 start = c_start[0] - PAD + jt * HALF // 2
@@ -166,30 +168,32 @@ def tile_list_pnet_bias_kernel(
 
         early = {(jt, g): sums(2 * g + jt, jt, g=g) for g in range(2) for jt in FOLDED}
         early[2, 0] = sums(6, 2, g=0)
+        second = {3: sums(5, 3, g=1)}
         early[1, 2] = sums(4, 1, g=2)
+        third = {2: sums(7, 2, g=2)}
 
         wc_dealt = wc_grouped[:].rearrange("p (t h m i) -> p h m i t", t=PACK, h=2, i=PACK)
         for h in range(2):
             nc.scalar.copy(out=wc_dealt[:, h], in_=wc_raw[h][:].rearrange("p i (m t) -> p m i t", t=PACK))
         nc.vector.quantize_mx(out=wc_codes[:].bitcast(FP8X4), scales=wc_plane[:], in_=wc_grouped[:])
-        round_c(0)
-        quantise_c(0)
         first_copy(0, early[0, 0])
         early[3, 0] = sums(0, 3, g=0)
+        round_c(0)
         first_copy(1, early[1, 0])
         maximum(0, early[0, 1])
+        second[2] = sums(2, 2, g=1)
+        quantise_c(0)
         nc.gpsimd.tensor_scalar(
             c_grouped[1][:].rearrange("p (j t) -> p j t", t=PACK), c_raw[1][:].rearrange("p t j -> p j t"), 1.0, 0.0, op0=MULT, op1=ADD
         )
-        own_banks = (7, 5)
-        own_sums = sums(own_banks[0], 0, with_own=True)
+        own_banks = (3, 6)
         early[0, 2] = sums(1, 0, g=2)
         maximum(1, early[1, 1])
         for jt in TURNED:
             first_copy(jt, early[jt, 0])
-        own_copy(0, own_sums)
-        own_copy(1, sums(own_banks[1], 1, with_own=True))
-        second = {jt: sums(jt, jt, g=1) for jt in TURNED}
+        for jt in FOLDED:
+            own_copy(jt, sums(own_banks[jt], jt, with_own=True))
+        third[3] = sums(0, 3, g=2)
         for jt in FOLDED:
             maximum(jt, early[jt, 2])
         quantise_c(1)
@@ -198,16 +202,14 @@ def tile_list_pnet_bias_kernel(
             three[jt] = rounded.tile(layout(jt), BF16, name=f"three{jt}", align_bytes=64, offset=jt * HALF // 4)
             nc.gpsimd.tensor_tensor(out=three[jt][:], in0=pooled[jt][:], in1=own[jt][:], op=ADD)
         folded = {}
-        third = {}
         for jt in TURNED:
-            third[jt] = sums((6, 0)[jt - 2], jt, g=2)
             own_copy(jt, sums(own_banks[jt - 2], jt, with_own=True))
         for jt in TURNED:
             maximum(jt, second[jt])
         fourth = {}
         for jt in FOLDED:
             folded[jt] = sums((1, 4)[jt], jt, g=3, with_own=True)
-            fourth[jt + 2] = sums(jt + 2, jt + 2, g=3)
+            fourth[jt + 2] = sums((2, 5)[jt], jt + 2, g=3)
         last = {}
         for jt in FOLDED:
             last[jt] = keep.tile(layout(jt), BF16, name=f"last{jt}", align_bytes=64)
@@ -224,9 +226,11 @@ def tile_list_pnet_bias_kernel(
         h_codes = keep.tile([P, J], U32, name="h_codes", align_bytes=64)
         h_plane = keep.tile([P, J], U8, name="h_plane", align_bytes=64)
         for jt in TURNED:
-            maximum(jt, fourth[jt])
-            for t in range(PACK):
-                nc.tensor.matmul(summed[jt][:, t, :], pooled[jt][:, t, :], identity[:], start=False, stop=t == PACK - 1, is_transpose=True)
+            for half in range(2):
+                slots = slice(2 * half, 2 * half + 2)
+                nc.vector.tensor_tensor(out=pooled[jt][:, slots], in0=pooled[jt][:, slots], in1=fourth[jt][:, slots], op=MAX)
+                for t in range(2 * half, 2 * half + 2):
+                    nc.tensor.matmul(summed[jt][:, t, :], pooled[jt][:, t, :], identity[:], start=False, stop=t == PACK - 1, is_transpose=True)
             nc.scalar.activation(out=h_grouped[1][:, jt - 2], in_=summed[jt][:].rearrange("p t j -> p j t"), func=ACT.Relu)
         for jt in FOLDED:
             nc.vector.tensor_tensor(out=h_grouped[0][:, jt], in0=last[jt][:], in1=three[jt][:], op=MAX)
@@ -266,6 +270,6 @@ def tile_list_pnet_bias_kernel(
         finish(0, 2 * P, (1, 4))
         for h in range(2):
             nc.sync.dma_start(out=out_rows[:, h, : J // 2], in_=results[h, 0][:])
-        finish(2, P, (6, 0))
+        finish(2, P, (7, 0))
         for h, queue in enumerate((nc.scalar, nc.sync)):
             queue.dma_start(out=out_rows[:, h, J // 2 :], in_=results[h, 1][:])

@@ -23,6 +23,7 @@ P = 128
 PACK = 4
 TILES = J // P
 FIRST_ROW = P - 16
+WEIGHT_ROW = P // 2 - 16
 FOLDED = (0, 1)
 TURNED = (2, 3)
 HALF = 4 * PACK * J // 2
@@ -33,9 +34,9 @@ def columns(tile, width=P):
     return slice(tile * width, (tile + 1) * width)
 
 
-def move_home(nc, plane, rows):
+def move_home(nc, plane, rows, first_row):
     for r in range(4):
-        nc.sync.dma_start(out=plane[r:P:32, :].bitcast(I32), in_=rows[FIRST_ROW + r : P : 4, :].bitcast(I32))
+        nc.sync.dma_start(out=plane[r:P:32, :].bitcast(I32), in_=rows[first_row + r : first_row + 16 : 4, :].bitcast(I32))
 
 
 def tile_list_pnet_bias_kernel(
@@ -52,41 +53,41 @@ def tile_list_pnet_bias_kernel(
 
         offsets = keep.tile([P, G * J // 16], U16, name="offsets")
         picked_rows = keep.tile([P, G * J], U8, name="picked_rows", align_bytes=64)
-        picked_plane = keep.tile([P, G * J], U8, name="picked_plane", align_bytes=64)
         table = keep.tile([P, T], I32, name="table", align_bytes=64)
         w_codes = keep.tile([P, R], I32, name="w_codes", align_bytes=64)
         weight_rows = keep.tile([P, R + N], U8, name="weight_rows", align_bytes=64)
         weight_plane = keep.tile([P, R + N], U8, name="weight_plane", align_bytes=64)
         w_rows = wc_side.tile([P, R], U8, name="w_rows", align_bytes=64, offset=HALF - R // 2)
         wc_raw = [wc_side.tile([P, PACK, R // 2], F32, name=f"wc_raw{h}", align_bytes=64, offset=h * HALF) for h in range(2)]
-        tab_rows = c_side.tile([P, T], U8, name="tab_rows", align_bytes=64, offset=HALF - PAD)
+        tab_rows = c_side.tile([P, T], U8, name="tab_rows", align_bytes=64, offset=HALF - PAD // 4)
         wd_codes = c_side.tile([P, 2 * N], U8, name="wd_codes", align_bytes=64, offset=HALF)
         bias = c_side.tile([P, N // P], F32, name="bias", align_bytes=64, offset=HALF + 3 * N)
-        c_start = [HALF + 2 * PAD, 0]
+        c_start = [HALF + PAD + G * J, 0]
         c_raw = [c_side.tile([P, PACK, J // 2], F32, name=f"c_raw{h}", align_bytes=64, offset=c_start[h]) for h in range(2)]
 
         identity = keep.tile([P, P], F32, name="identity", align_bytes=64)
         make_identity(nc, identity[:])
-        nc.vector.memset(w_rows[:FIRST_ROW, :].bitcast(I32), 0)
+        nc.vector.memset(w_rows[:WEIGHT_ROW, :].bitcast(I32), 0)
+        nc.vector.memset(w_rows[P // 2 :, :].bitcast(I32), 0)
         nc.vector.memset(tab_rows[:FIRST_ROW, :].bitcast(I32), 0)
         nc.vector.memset(weight_plane[:].bitcast(I32), 0)
-        nc.vector.memset(picked_plane[:].bitcast(I32), 0)
 
-        nc.scalar.dma_start(out=weight_rows[FIRST_ROW:, R:].bitcast(I32), in_=wd_scales[0].bitcast(I32))
-        nc.scalar.dma_start(out=w_rows[FIRST_ROW:, :].bitcast(I32), in_=w_scales[0].bitcast(I32))
-        nc.sync.dma_start(out=tab_rows[FIRST_ROW:, :].bitcast(I32), in_=tab_scales[0].bitcast(I32))
+        nc.scalar.dma_start(out=tab_rows[FIRST_ROW:, :].bitcast(I32), in_=tab_scales[0].bitcast(I32))
+        nc.sync.dma_start(out=w_rows[WEIGHT_ROW : P // 2, :].bitcast(I32), in_=w_scales[0].bitcast(I32))
         nc.sync.dma_start(offsets[:], offs)
+        nc.sync.dma_start(out=weight_rows[WEIGHT_ROW : P // 2, R:].bitcast(I32), in_=wd_scales[0].bitcast(I32))
         nc.sync.dma_start(out=w_codes[:], in_=w_words[0].rearrange("p r i -> p (r i)").bitcast(I32))
         nc.sync.dma_start(out=table[:], in_=tab_words[0].rearrange("p t i -> p (t i)").bitcast(I32))
 
         nc.vector.tensor_copy(weight_rows[:, :R].rearrange("p (t m) -> p t m", t=PACK), w_rows[:].rearrange("p (m t) -> p t m", t=PACK))
-        move_home(nc, weight_plane, weight_rows)
+        move_home(nc, weight_plane, weight_rows, WEIGHT_ROW)
         wc_rows = wc.rearrange("(p t) r -> p t r", t=PACK)
         for h in range(2):
             nc.sync.dma_start(out=wc_raw[h][:], in_=wc_rows[:, :, columns(h, R // 2)])
 
         nc.vector.tensor_copy(picked_rows[:], tab_rows[:].indirect(offsets[:]))
-        move_home(nc, picked_plane, picked_rows)
+        picked_plane = c_side.tile([P, G * J], U8, name="picked_plane", align_bytes=64, offset=HALF + PAD)
+        move_home(nc, picked_plane, picked_rows, FIRST_ROW)
         c_rows = c.rearrange("(p t) j -> p t j", t=PACK)
         for h in range(2):
             nc.sync.dma_start(out=c_raw[h][:], in_=c_rows[:, :, columns(h, J // 2)])
@@ -264,9 +265,8 @@ def tile_list_pnet_bias_kernel(
             for h, add_bias in enumerate((add_bias_scalar, add_bias_vector)):
                 add_bias(results[h, first_tile // 2][:], y[h][:], h)
 
-        quantise(0, 2)
-        quantise(2, 1)
-        quantise(3, 1)
+        for jt in range(TILES):
+            quantise(jt, 1)
         finish(0, 2 * P, (1, 4))
         for h in range(2):
             nc.sync.dma_start(out=out_rows[:, h, : J // 2], in_=results[h, 0][:])

@@ -49,13 +49,14 @@ def tile_list_pnet_bias_kernel(
         c_side = ctx.enter_context(tc.tile_pool(name="c_side", bufs=1))
         rounded = ctx.enter_context(tc.tile_pool(name="rounded", bufs=1))
         ending = ctx.enter_context(tc.tile_pool(name="ending", bufs=1))
+        words = ctx.enter_context(tc.tile_pool(name="words", bufs=1))
         psum = ctx.enter_context(tc.psum_pool(name="psum", bufs=1))
 
         offsets = keep.tile([P, G * J // 16], U16, name="offsets")
         picked_rows = keep.tile([P, G * J], U8, name="picked_rows", align_bytes=64)
         table = keep.tile([P, T], I32, name="table", align_bytes=64)
         w_codes = keep.tile([P, R], I32, name="w_codes", align_bytes=64)
-        weight_rows = keep.tile([P, R + N], U8, name="weight_rows", align_bytes=64)
+        weight_rows = words.tile([P, R + N], U8, name="weight_rows", align_bytes=64, offset=4 * J - N)
         weight_plane = keep.tile([P, R + N], U8, name="weight_plane", align_bytes=64)
         w_rows = wc_side.tile([P, R], U8, name="w_rows", align_bytes=64, offset=HALF - R // 2)
         wc_raw = [wc_side.tile([P, PACK, R // 2], F32, name=f"wc_raw{h}", align_bytes=64, offset=h * HALF) for h in range(2)]
@@ -75,9 +76,9 @@ def tile_list_pnet_bias_kernel(
         nc.scalar.dma_start(out=tab_rows[FIRST_ROW:, :].bitcast(I32), in_=tab_scales[0].bitcast(I32))
         nc.sync.dma_start(out=w_rows[WEIGHT_ROW : P // 2, :].bitcast(I32), in_=w_scales[0].bitcast(I32))
         nc.sync.dma_start(offsets[:], offs)
-        nc.sync.dma_start(out=weight_rows[WEIGHT_ROW : P // 2, R:].bitcast(I32), in_=wd_scales[0].bitcast(I32))
-        nc.sync.dma_start(out=w_codes[:], in_=w_words[0].rearrange("p r i -> p (r i)").bitcast(I32))
         nc.sync.dma_start(out=table[:], in_=tab_words[0].rearrange("p t i -> p (t i)").bitcast(I32))
+        nc.sync.dma_start(out=w_codes[:], in_=w_words[0].rearrange("p r i -> p (r i)").bitcast(I32))
+        nc.scalar.dma_start(out=weight_rows[WEIGHT_ROW : P // 2, R:].bitcast(I32), in_=wd_scales[0].bitcast(I32))
 
         nc.vector.tensor_copy(weight_rows[:, :R].rearrange("p (t m) -> p t m", t=PACK), w_rows[:].rearrange("p (m t) -> p t m", t=PACK))
         move_home(nc, weight_plane, weight_rows, WEIGHT_ROW)
@@ -95,14 +96,17 @@ def tile_list_pnet_bias_kernel(
         with nc.allow_non_contiguous_dma(reason="one bias value a partition"):
             nc.sync.dma_start(out=bias[:], in_=b.rearrange("(h p) -> p h", p=P))
 
+        def gather_words(tile, first, count):
+            nc.vector.tensor_copy(tile[:], table[:].bitcast(U32).indirect(offsets[:, first * J // 16 : (first + count) * J // 16]))
+            return [tile[:, columns(n, J)] for n in range(count)]
+
+        picked = gather_words(keep.tile([P, J], U32, name="picked0", align_bytes=64), 0, 1)
         w_dealt = keep.tile([P, R], I32, name="w_dealt", align_bytes=64)
         nc.vector.tensor_copy(
             w_dealt[:].rearrange("p (t m i) -> p m t i", t=PACK, i=4), w_codes[:].rearrange("p (m i t) -> p m t i", t=PACK, i=4)
         )
-        picked_pairs = [keep.tile([P, 2 * J], U32, name=f"picked{n}", align_bytes=64) for n in range(2)]
-        for n in range(2):
-            nc.vector.tensor_copy(picked_pairs[n][:], table[:].bitcast(U32).indirect(offsets[:, columns(n, 2 * J // 16)]))
-        picked = [picked_pairs[g // 2][:, columns(g % 2, J)] for g in range(G)]
+        picked.extend(gather_words(words.tile([P, J], U32, name="picked1", align_bytes=64, offset=0), 1, 1))
+        picked.extend(gather_words(words.tile([P, 2 * J], U32, name="picked2", align_bytes=64, offset=4 * J), 2, 2))
 
         wc_grouped = keep.tile([P, PACK * R], BF16, name="wc_grouped", align_bytes=64)
         wc_codes = keep.tile([P, R], U32, name="wc_codes", align_bytes=64)

@@ -247,33 +247,34 @@ def tile_list_pnet_bias_kernel(
 
         out_rows = out.rearrange("(h p) j -> p h j", p=P)
 
+        def second_layer(target, h, cols):
+            nc.tensor.matmul_mx(
+                out=target, lhsT=wd_codes[:, columns(h, 2 * P)].bitcast(FP4X4), lhsT_scale=weight_plane[:, R + h * P : R + (h + 1) * P],
+                rhs=h_codes[:, cols].bitcast(FP8X4), rhs_scale=h_plane[:, cols], start=True, stop=True,
+            )
+
         def add_bias_scalar(result, y, h):
             nc.scalar.activation(out=result, in_=y, func=ACT.Identity, bias=bias[:, h : h + 1])
 
         def add_bias_vector(result, y, h):
             nc.vector.tensor_scalar(result, y, bias[:, h : h + 1], None, op0=ADD)
 
-        results = {(h, pair): keep.tile([P, J // 2], F32, name=f"result{h}{pair}", align_bytes=64) for h, pair in ((0, 0), (0, 1), (1, 1))}
-        results[1, 0] = ending.tile([P, J // 2], F32, name="result10", align_bytes=64, offset=HALF // 2)
-
-        def finish(first_tile, width, banks):
-            y = [psum.tile([P, 2 * P], F32, name="bank", tag=f"bank{banks[h]}") for h in range(2)]
-            for start in range(0, 2 * P, width):
-                cols = slice(first_tile * P + start, first_tile * P + start + width)
-                for h in range(2):
-                    nc.tensor.matmul_mx(
-                        out=y[h][:, start : start + width], lhsT=wd_codes[:, columns(h, 2 * P)].bitcast(FP4X4),
-                        lhsT_scale=weight_plane[:, R + h * P : R + (h + 1) * P],
-                        rhs=h_codes[:, cols].bitcast(FP8X4), rhs_scale=h_plane[:, cols], start=True, stop=True,
-                    )
-            for h, add_bias in enumerate((add_bias_scalar, add_bias_vector)):
-                add_bias(results[h, first_tile // 2][:], y[h][:], h)
-
         for jt in range(TILES):
             quantise(jt, 1)
-        finish(0, 2 * P, (1, 4))
         for h in range(2):
-            nc.sync.dma_start(out=out_rows[:, h, : J // 2], in_=results[h, 0][:])
-        finish(2, P, (7, 0))
-        for h, queue in enumerate((nc.scalar, nc.sync)):
-            queue.dma_start(out=out_rows[:, h, J // 2 :], in_=results[h, 1][:])
+            y = psum.tile([P, 2 * P], F32, name="bank", tag=f"bank{(1, 4)[h]}")
+            second_layer(y[:], h, columns(0, 2 * P))
+            result = keep.tile([P, 2 * P], F32, name=f"result{h}", align_bytes=64)
+            add_bias_scalar(result[:], y[:], h)
+            nc.sync.dma_start(out=out_rows[:, h, columns(0, 2 * P)], in_=result[:])
+        results = {
+            2: ending.tile([P, 2, P], F32, name="result2", align_bytes=64, offset=HALF // 2),
+            3: keep.tile([P, 2, P], F32, name="result3", align_bytes=64),
+        }
+        for jt, add_bias, queue in ((2, add_bias_vector, nc.sync), (3, add_bias_scalar, nc.scalar)):
+            y = psum.tile([P, 2, P], F32, name="bank", tag=f"bank{(7, 0)[jt - 2]}")
+            for h in range(2):
+                second_layer(y[:, h], h, columns(jt))
+            for h in range(2):
+                add_bias(results[jt][:, h], y[:, h], h)
+            queue.dma_start(out=out_rows[:, :, columns(jt)], in_=results[jt][:])

@@ -115,31 +115,37 @@ def tile_list_pnet_bias_kernel(
         c_codes = [keep.tile([P, J // 2], U32, name=f"c_codes{h}", align_bytes=64) for h in range(2)]
         c_plane = [keep.tile([P, J // 2], U8, name=f"c_plane{h}", align_bytes=64) for h in range(2)]
 
-        def sums(index, jt, g=None, with_own=False):
-            bank = psum.tile([P, PACK, P], F32, name="bank", tag=f"bank{index}")
-            passes = []
-            if g is not None:
-                passes.append((w_dealt[:], weight_plane[:, :R], picked[g][:, columns(jt)], picked_plane[:, columns(g * TILES + jt)]))
-            if with_own:
-                passes.append((wc_codes[:], wc_plane[:], c_codes[jt // 2][:, columns(jt % 2)], c_plane[jt // 2][:, columns(jt % 2)]))
-            if jt in TURNED:
-                moving, moving_plane, codes, plane = passes[0]
+        def sums(index, unit, g=None, with_own=False):
+            if unit in TURNED:
+                bank = psum.tile([P, PACK, P], F32, name="bank", tag=f"bank{index}")
+                if with_own:
+                    moving, moving_plane, codes, plane = wc_codes[:], wc_plane[:], c_codes[1][:, columns(unit % 2)], c_plane[1][:, columns(unit % 2)]
+                else:
+                    moving, moving_plane = w_dealt[:], weight_plane[:, :R]
+                    codes, plane = picked[g][:, columns(unit)], picked_plane[:, columns(g * TILES + unit)]
                 nc.tensor.matmul_mx(
                     out=bank[:].rearrange("p t m -> p (t m)"), lhsT=codes.bitcast(FP8X4), lhsT_scale=plane,
                     rhs=moving.bitcast(FP8X4), rhs_scale=moving_plane, start=True, stop=True,
                 )
                 return bank[:]
+            bank = psum.tile([P, 2, 2 * P], F32, name="bank", tag=f"bank{index}")
+            passes = []
+            if g is not None:
+                passes.append((w_dealt[:], weight_plane[:, :R], picked[g][:, : 2 * P], picked_plane[:, columns(2 * g, 2 * P)]))
+            if with_own:
+                passes.append((wc_codes[:], wc_plane[:], c_codes[0][:], c_plane[0][:]))
             for n, (codes, plane, moving, moving_plane) in enumerate(passes):
-                for t in range(PACK):
+                for e in range(2):
+                    t = 2 * unit + e
                     nc.tensor.matmul_mx(
-                        out=bank[:, t, :], lhsT=codes[:, columns(t)].bitcast(FP8X4), lhsT_scale=plane[:, columns(t)],
+                        out=bank[:, e, :], lhsT=codes[:, columns(t)].bitcast(FP8X4), lhsT_scale=plane[:, columns(t)],
                         rhs=moving.bitcast(FP8X4), rhs_scale=moving_plane,
-                        start=n == 0 and t == 0, stop=n == len(passes) - 1 and t == PACK - 1,
+                        start=n == 0 and e == 0, stop=n == len(passes) - 1 and e == 1,
                     )
-            return bank[:].rearrange("p t j -> p j t")
+            return bank[:].rearrange("p e j -> p j e")
 
-        def layout(jt):
-            return [P, PACK, P] if jt in TURNED else [P, P, PACK]
+        def layout(unit):
+            return [P, PACK, P] if unit in TURNED else [P, 2 * P, 2]
 
         def round_c(h):
             nc.scalar.copy(
@@ -202,10 +208,9 @@ def tile_list_pnet_bias_kernel(
         for jt in FOLDED:
             maximum(jt, early[jt, 2])
         quantise_c(1)
-        three = {}
+        three = rounded.tile([P, 2, 2 * P, 2], BF16, name="three", align_bytes=64, offset=0)
         for jt in FOLDED:
-            three[jt] = rounded.tile(layout(jt), BF16, name=f"three{jt}", align_bytes=64, offset=jt * HALF // 4)
-            nc.gpsimd.tensor_tensor(out=three[jt][:], in0=pooled[jt][:], in1=own[jt][:], op=ADD)
+            nc.gpsimd.tensor_tensor(out=three[:, jt], in0=pooled[jt][:], in1=own[jt][:], op=ADD)
         folded = {}
         for jt in TURNED:
             own_copy(jt, sums(own_banks[jt - 2], jt, with_own=True))
@@ -215,10 +220,9 @@ def tile_list_pnet_bias_kernel(
         for jt in FOLDED:
             folded[jt] = sums((1, 4)[jt], jt, g=3, with_own=True)
             fourth[jt + 2] = sums((2, 5)[jt], jt + 2, g=3)
-        last = {}
+        last = keep.tile([P, 2, 2 * P, 2], BF16, name="last", align_bytes=64)
         for jt in FOLDED:
-            last[jt] = keep.tile(layout(jt), BF16, name=f"last{jt}", align_bytes=64)
-            nc.scalar.activation(out=last[jt][:], in_=folded[jt], func=ACT.Relu)
+            nc.scalar.activation(out=last[:, jt], in_=folded[jt], func=ACT.Relu)
         summed = {}
         for jt in TURNED:
             summed[jt] = psum.tile([P, PACK, P], F32, name="bank", tag=f"bank{own_banks[jt - 2]}")
@@ -238,7 +242,12 @@ def tile_list_pnet_bias_kernel(
                     nc.tensor.matmul(summed[jt][:, t, :], pooled[jt][:, t, :], identity[:], start=False, stop=t == PACK - 1, is_transpose=True)
             nc.scalar.activation(out=h_grouped[1][:, jt - 2], in_=summed[jt][:].rearrange("p t j -> p j t"), func=ACT.Relu)
         for jt in FOLDED:
-            nc.vector.tensor_tensor(out=h_grouped[0][:, jt], in0=last[jt][:], in1=three[jt][:], op=MAX)
+            nc.vector.tensor_tensor(
+                out=h_grouped[0][:, jt].rearrange("p j (u e) -> p j u e", e=2),
+                in0=last[:, :, columns(jt), :].rearrange("p u j e -> p j u e"),
+                in1=three[:, :, columns(jt), :].rearrange("p u j e -> p j u e"),
+                op=MAX,
+            )
 
         def quantise(first_tile, count):
             cols = slice(first_tile * P, (first_tile + count) * P)

@@ -49,14 +49,13 @@ def tile_list_pnet_bias_kernel(
         c_side = ctx.enter_context(tc.tile_pool(name="c_side", bufs=1))
         rounded = ctx.enter_context(tc.tile_pool(name="rounded", bufs=1))
         ending = ctx.enter_context(tc.tile_pool(name="ending", bufs=1))
-        words = ctx.enter_context(tc.tile_pool(name="words", bufs=1))
         psum = ctx.enter_context(tc.psum_pool(name="psum", bufs=1))
 
         offsets = keep.tile([P, G * J // 16], U16, name="offsets")
         picked_rows = keep.tile([P, G * J], U8, name="picked_rows", align_bytes=64)
         table = keep.tile([P, T], I32, name="table", align_bytes=64)
-        w_codes = keep.tile([P, R], I32, name="w_codes", align_bytes=64)
-        weight_rows = words.tile([P, R + N], U8, name="weight_rows", align_bytes=64, offset=4 * J - N)
+        w_codes = keep.tile([P, R], U32, name="w_codes", align_bytes=64)
+        weight_rows = keep.tile([P, R + N], U8, name="weight_rows", align_bytes=64)
         weight_plane = keep.tile([P, R + N], U8, name="weight_plane", align_bytes=64)
         w_rows = wc_side.tile([P, R], U8, name="w_rows", align_bytes=64, offset=HALF - R // 2)
         wc_raw = [wc_side.tile([P, PACK, R // 2], F32, name=f"wc_raw{h}", align_bytes=64, offset=h * HALF) for h in range(2)]
@@ -77,7 +76,7 @@ def tile_list_pnet_bias_kernel(
         nc.sync.dma_start(out=w_rows[WEIGHT_ROW : P // 2, :].bitcast(I32), in_=w_scales[0].bitcast(I32))
         nc.sync.dma_start(offsets[:], offs)
         nc.sync.dma_start(out=table[:], in_=tab_words[0].rearrange("p t i -> p (t i)").bitcast(I32))
-        nc.sync.dma_start(out=w_codes[:], in_=w_words[0].rearrange("p r i -> p (r i)").bitcast(I32))
+        nc.sync.dma_start(out=w_codes[:].bitcast(I32), in_=w_words[0].rearrange("p r i -> p (r i)").bitcast(I32))
         nc.scalar.dma_start(out=weight_rows[WEIGHT_ROW : P // 2, R:].bitcast(I32), in_=wd_scales[0].bitcast(I32))
 
         nc.vector.tensor_copy(weight_rows[:, :R].rearrange("p (t m) -> p t m", t=PACK), w_rows[:].rearrange("p (m t) -> p t m", t=PACK))
@@ -101,12 +100,12 @@ def tile_list_pnet_bias_kernel(
             return [tile[:, columns(n, J)] for n in range(count)]
 
         picked = gather_words(keep.tile([P, J], U32, name="picked0", align_bytes=64), 0, 1)
-        w_dealt = keep.tile([P, R], I32, name="w_dealt", align_bytes=64)
-        nc.vector.tensor_copy(
-            w_dealt[:].rearrange("p (t m i) -> p m t i", t=PACK, i=4), w_codes[:].rearrange("p (m i t) -> p m t i", t=PACK, i=4)
+        w_dealt = keep.tile([P, R], U32, name="w_dealt", align_bytes=64)
+        nc.scalar.copy(
+            out=w_dealt[:].rearrange("p (t m i) -> p m t i", t=PACK, i=4), in_=w_codes[:].rearrange("p (m i t) -> p m t i", t=PACK, i=4)
         )
-        picked.extend(gather_words(words.tile([P, J], U32, name="picked1", align_bytes=64, offset=0), 1, 1))
-        picked.extend(gather_words(words.tile([P, 2 * J], U32, name="picked2", align_bytes=64, offset=4 * J), 2, 2))
+        picked.extend(gather_words(keep.tile([P, J], U32, name="picked1", align_bytes=64), 1, 1))
+        picked.extend(gather_words(keep.tile([P, 2 * J], U32, name="picked2", align_bytes=64), 2, 2))
 
         wc_grouped = keep.tile([P, PACK * R], BF16, name="wc_grouped", align_bytes=64)
         wc_codes = keep.tile([P, R], U32, name="wc_codes", align_bytes=64)

@@ -58,12 +58,14 @@ def tile_list_pnet_bias_kernel(
         weight_rows = keep.tile([P, R + N], U8, name="weight_rows", align_bytes=64)
         weight_plane = keep.tile([P, R + N], U8, name="weight_plane", align_bytes=64)
         w_rows = wc_side.tile([P, R], U8, name="w_rows", align_bytes=64, offset=HALF - R // 2)
-        wc_raw = [wc_side.tile([P, PACK, R // 2], F32, name=f"wc_raw{h}", align_bytes=64, offset=h * HALF) for h in range(2)]
-        tab_rows = c_side.tile([P, T], U8, name="tab_rows", align_bytes=64, offset=HALF - PAD // 4)
-        wd_codes = c_side.tile([P, 2 * N], U8, name="wd_codes", align_bytes=64, offset=HALF)
-        bias = c_side.tile([P, N // P], F32, name="bias", align_bytes=64, offset=HALF + 3 * N)
-        c_start = [HALF + PAD + G * J, 0]
-        c_raw = [c_side.tile([P, PACK, J // 2], F32, name=f"c_raw{h}", align_bytes=64, offset=c_start[h]) for h in range(2)]
+        late_raw = c_side.tile([P, PACK * J], F32, name="late_raw", align_bytes=64, offset=0)
+        late = [late_raw[:, columns(h, PACK * J // 2)].rearrange("p (t j) -> p t j", t=PACK) for h in range(2)]
+        wc_raw = [wc_side.tile([P, PACK, R // 2], F32, name="wc_raw0", align_bytes=64, offset=0)[:], late[0]]
+        tab_rows = c_side.tile([P, T], U8, name="tab_rows", align_bytes=64, offset=2 * HALF - PAD // 4)
+        wd_codes = c_side.tile([P, 2 * N], U8, name="wd_codes", align_bytes=64, offset=2 * HALF)
+        bias = c_side.tile([P, N // P], F32, name="bias", align_bytes=64, offset=2 * HALF + 3 * N)
+        c_start = [2 * HALF + PAD + G * J, 0]
+        c_raw = [c_side.tile([P, PACK, J // 2], F32, name="c_raw0", align_bytes=64, offset=c_start[0])[:], late[1]]
 
         identity = keep.tile([P, P], F32, name="identity", align_bytes=64)
         make_identity(nc, identity[:])
@@ -82,15 +84,15 @@ def tile_list_pnet_bias_kernel(
         nc.vector.tensor_copy(weight_rows[:, :R].rearrange("p (t m) -> p t m", t=PACK), w_rows[:].rearrange("p (m t) -> p t m", t=PACK))
         move_home(nc, weight_plane, weight_rows, WEIGHT_ROW)
         wc_rows = wc.rearrange("(p t) r -> p t r", t=PACK)
-        for h in range(2):
-            nc.sync.dma_start(out=wc_raw[h][:], in_=wc_rows[:, :, columns(h, R // 2)])
+        nc.sync.dma_start(out=wc_raw[0], in_=wc_rows[:, :, columns(0, R // 2)])
 
         nc.vector.tensor_copy(picked_rows[:], tab_rows[:].indirect(offsets[:]))
-        picked_plane = c_side.tile([P, G * J], U8, name="picked_plane", align_bytes=64, offset=HALF + PAD)
+        picked_plane = c_side.tile([P, G * J], U8, name="picked_plane", align_bytes=64, offset=2 * HALF + PAD)
         move_home(nc, picked_plane, picked_rows, FIRST_ROW)
+        nc.sync.dma_start(out=wc_raw[1], in_=wc_rows[:, :, columns(1, R // 2)])
         c_rows = c.rearrange("(p t) j -> p t j", t=PACK)
         for h in range(2):
-            nc.sync.dma_start(out=c_raw[h][:], in_=c_rows[:, :, columns(h, J // 2)])
+            nc.sync.dma_start(out=c_raw[h], in_=c_rows[:, :, columns(h, J // 2)])
         nc.sync.dma_start(out=wd_codes[:].bitcast(I32), in_=wd_words[0].bitcast(I32))
         with nc.allow_non_contiguous_dma(reason="one bias value a partition"):
             nc.sync.dma_start(out=bias[:], in_=b.rearrange("(h p) -> p h", p=P))
@@ -149,7 +151,7 @@ def tile_list_pnet_bias_kernel(
         def round_c(h):
             nc.scalar.copy(
                 out=c_grouped[h][:].rearrange("p (j i t) -> p j t i", i=4, t=PACK),
-                in_=c_raw[h][:].rearrange("p t (j i) -> p j t i", i=4),
+                in_=c_raw[h].rearrange("p t (j i) -> p j t i", i=4),
             )
 
         def quantise_c(h):
@@ -159,7 +161,7 @@ def tile_list_pnet_bias_kernel(
 
         def first_copy(jt, bank):
             if jt == 0:
-                pooled[jt] = wc_side.tile(layout(jt), F32, name="pooled0", align_bytes=64, offset=HALF)
+                pooled[jt] = keep.tile(layout(jt), F32, name="pooled0", align_bytes=64)
             elif jt == 3:
                 pooled[jt] = keep.tile(layout(jt), F32, name="pooled3", align_bytes=64)
             else:
@@ -183,10 +185,10 @@ def tile_list_pnet_bias_kernel(
         third = {2: sums(7, 2, g=2)}
 
         wc_dealt = wc_grouped[:].rearrange("p (t h m i) -> p h m i t", t=PACK, h=2, i=PACK)
-        for h in range(2):
-            nc.scalar.copy(out=wc_dealt[:, h], in_=wc_raw[h][:].rearrange("p i (m t) -> p m i t", t=PACK))
-        nc.vector.quantize_mx(out=wc_codes[:].bitcast(FP8X4), scales=wc_plane[:], in_=wc_grouped[:])
+        nc.scalar.copy(out=wc_dealt[:, 0], in_=wc_raw[0].rearrange("p i (m t) -> p m i t", t=PACK))
         first_copy(0, early[0, 0])
+        nc.scalar.copy(out=wc_dealt[:, 1], in_=wc_raw[1].rearrange("p i (m t) -> p m i t", t=PACK))
+        nc.vector.quantize_mx(out=wc_codes[:].bitcast(FP8X4), scales=wc_plane[:], in_=wc_grouped[:])
         early[3, 0] = sums(0, 3, g=0)
         round_c(0)
         first_copy(1, early[1, 0])
@@ -194,7 +196,7 @@ def tile_list_pnet_bias_kernel(
         second[2] = sums(2, 2, g=1)
         quantise_c(0)
         nc.gpsimd.tensor_scalar(
-            c_grouped[1][:].rearrange("p (j t) -> p j t", t=PACK), c_raw[1][:].rearrange("p t j -> p j t"), 1.0, 0.0, op0=MULT, op1=ADD
+            c_grouped[1][:].rearrange("p (j t) -> p j t", t=PACK), c_raw[1].rearrange("p t j -> p j t"), 1.0, 0.0, op0=MULT, op1=ADD
         )
         own_banks = (3, 6)
         early[0, 2] = sums(1, 0, g=2)

@@ -65,7 +65,8 @@ def tile_list_pnet_bias_kernel(
         wd_codes = c_side.tile([P, 2 * N], U8, name="wd_codes", align_bytes=64, offset=2 * HALF)
         bias = c_side.tile([P, N // P], F32, name="bias", align_bytes=64, offset=2 * HALF + 3 * N)
         c_start = [2 * HALF + PAD + G * J, 0]
-        c_raw = [c_side.tile([P, PACK, J // 2], F32, name="c_raw0", align_bytes=64, offset=c_start[0])[:], late[1]]
+        c_wide = c_side.tile([P, PACK * J // 2 + 16], F32, name="c_raw0", align_bytes=64, offset=c_start[0])
+        c_raw = [c_wide[:, : PACK * J // 2].rearrange("p (t j) -> p t j", t=PACK), late[1]]
 
         identity = keep.tile([P, P], F32, name="identity", align_bytes=64)
         make_identity(nc, identity[:])
@@ -162,10 +163,8 @@ def tile_list_pnet_bias_kernel(
         def first_copy(jt, bank):
             if jt == 0:
                 pooled[jt] = keep.tile(layout(jt), F32, name="pooled0", align_bytes=64)
-            elif jt == 3:
-                pooled[jt] = keep.tile(layout(jt), F32, name="pooled3", align_bytes=64)
             else:
-                start = c_start[0] - PAD + jt * HALF // 2
+                start = c_start[0] + (jt - 1) * HALF // 2
                 pooled[jt] = c_side.tile(layout(jt), F32, name=f"pooled{jt}", align_bytes=64, offset=start)
             nc.scalar.copy(out=pooled[jt][:], in_=bank)
 

@@ -54,13 +54,13 @@ def tile_list_pnet_bias_kernel(
         offsets = keep.tile([P, G * J // 16], U16, name="offsets")
         picked_rows = keep.tile([P, G * J], U8, name="picked_rows", align_bytes=64)
         table = keep.tile([P, T], I32, name="table", align_bytes=64)
-        w_codes = keep.tile([P, R], U32, name="w_codes", align_bytes=64)
         weight_rows = keep.tile([P, R + N], U8, name="weight_rows", align_bytes=64)
         weight_plane = keep.tile([P, R + N], U8, name="weight_plane", align_bytes=64)
         w_rows = wc_side.tile([P, R], U8, name="w_rows", align_bytes=64, offset=HALF - R // 2)
         late_raw = c_side.tile([P, PACK * J], F32, name="late_raw", align_bytes=64, offset=0)
         late = [late_raw[:, columns(h, PACK * J // 2)].rearrange("p (t j) -> p t j", t=PACK) for h in range(2)]
         wc_raw = [wc_side.tile([P, PACK, R // 2], F32, name="wc_raw0", align_bytes=64, offset=0)[:], late[0]]
+        w_codes = wc_side.tile([P, R], U32, name="w_codes", align_bytes=64, offset=HALF)
         tab_rows = c_side.tile([P, T], U8, name="tab_rows", align_bytes=64, offset=2 * HALF - PAD // 4)
         wd_codes = c_side.tile([P, 2 * N], U8, name="wd_codes", align_bytes=64, offset=2 * HALF)
         bias = c_side.tile([P, N // P], F32, name="bias", align_bytes=64, offset=2 * HALF + 3 * N)
@@ -79,11 +79,11 @@ def tile_list_pnet_bias_kernel(
         nc.sync.dma_start(out=w_rows[WEIGHT_ROW : P // 2, :].bitcast(I32), in_=w_scales[0].bitcast(I32))
         nc.sync.dma_start(offsets[:], offs)
         nc.sync.dma_start(out=table[:], in_=tab_words[0].rearrange("p t i -> p (t i)").bitcast(I32))
-        nc.sync.dma_start(out=w_codes[:].bitcast(I32), in_=w_words[0].rearrange("p r i -> p (r i)").bitcast(I32))
         nc.scalar.dma_start(out=weight_rows[WEIGHT_ROW : P // 2, R:].bitcast(I32), in_=wd_scales[0].bitcast(I32))
 
         nc.vector.tensor_copy(weight_rows[:, :R].rearrange("p (t m) -> p t m", t=PACK), w_rows[:].rearrange("p (m t) -> p t m", t=PACK))
         move_home(nc, weight_plane, weight_rows, WEIGHT_ROW)
+        nc.sync.dma_start(out=w_codes[:].bitcast(I32), in_=w_words[0].rearrange("p r i -> p (r i)").bitcast(I32))
         wc_rows = wc.rearrange("(p t) r -> p t r", t=PACK)
         nc.sync.dma_start(out=wc_raw[0], in_=wc_rows[:, :, columns(0, R // 2)])
 

@@ -28,6 +28,7 @@ FOLDED = (0, 1)
 TURNED = (2, 3)
 HALF = 4 * PACK * J // 2
 PAD = HALF // 4
+EARLY = 5 * R // 8
 
 
 def columns(tile, width=P):
@@ -56,11 +57,11 @@ def tile_list_pnet_bias_kernel(
         table = keep.tile([P, T], I32, name="table", align_bytes=64)
         weight_rows = keep.tile([P, R + N], U8, name="weight_rows", align_bytes=64)
         weight_plane = keep.tile([P, R + N], U8, name="weight_plane", align_bytes=64)
-        w_rows = wc_side.tile([P, R], U8, name="w_rows", align_bytes=64, offset=HALF - R // 2)
+        w_rows = wc_side.tile([P, R], U8, name="w_rows", align_bytes=64, offset=4 * PACK * EARLY - R // 2)
         late_raw = c_side.tile([P, PACK * J], F32, name="late_raw", align_bytes=64, offset=0)
-        late = [late_raw[:, columns(h, PACK * J // 2)].rearrange("p (t j) -> p t j", t=PACK) for h in range(2)]
-        wc_raw = [wc_side.tile([P, PACK, R // 2], F32, name="wc_raw0", align_bytes=64, offset=0)[:], late[0]]
-        w_codes = wc_side.tile([P, R], U32, name="w_codes", align_bytes=64, offset=HALF)
+        late = [late_raw[:, cols].rearrange("p (t j) -> p t j", t=PACK) for cols in (slice(0, PACK * (R - EARLY)), columns(1, PACK * J // 2))]
+        wc_raw = [wc_side.tile([P, PACK, EARLY], F32, name="wc_raw0", align_bytes=64, offset=0)[:], late[0]]
+        w_codes = wc_side.tile([P, R], U32, name="w_codes", align_bytes=64, offset=4 * PACK * EARLY)
         tab_rows = c_side.tile([P, T], U8, name="tab_rows", align_bytes=64, offset=2 * HALF - PAD // 4)
         wd_codes = c_side.tile([P, 2 * N], U8, name="wd_codes", align_bytes=64, offset=2 * HALF)
         bias = c_side.tile([P, N // P], F32, name="bias", align_bytes=64, offset=2 * HALF + 3 * N)
@@ -85,12 +86,12 @@ def tile_list_pnet_bias_kernel(
         move_home(nc, weight_plane, weight_rows, WEIGHT_ROW)
         nc.sync.dma_start(out=w_codes[:].bitcast(I32), in_=w_words[0].rearrange("p r i -> p (r i)").bitcast(I32))
         wc_rows = wc.rearrange("(p t) r -> p t r", t=PACK)
-        nc.sync.dma_start(out=wc_raw[0], in_=wc_rows[:, :, columns(0, R // 2)])
+        nc.sync.dma_start(out=wc_raw[0], in_=wc_rows[:, :, :EARLY])
 
         nc.vector.tensor_copy(picked_rows[:], tab_rows[:].indirect(offsets[:]))
         picked_plane = c_side.tile([P, G * J], U8, name="picked_plane", align_bytes=64, offset=2 * HALF + PAD)
         move_home(nc, picked_plane, picked_rows, FIRST_ROW)
-        nc.sync.dma_start(out=wc_raw[1], in_=wc_rows[:, :, columns(1, R // 2)])
+        nc.sync.dma_start(out=wc_raw[1], in_=wc_rows[:, :, EARLY:])
         c_rows = c.rearrange("(p t) j -> p t j", t=PACK)
         for h in range(2):
             nc.sync.dma_start(out=c_raw[h], in_=c_rows[:, :, columns(h, J // 2)])
@@ -177,16 +178,16 @@ def tile_list_pnet_bias_kernel(
             own[jt] = keep.tile(layout(jt), F32, name=f"own{jt}", align_bytes=64)
             nc.scalar.copy(out=own[jt][:], in_=bank)
 
-        early = {(jt, g): sums(2 * g + jt, jt, g=g) for g in range(2) for jt in FOLDED}
+        early = {(jt, g): sums(2 * g + jt, jt, g=g) for jt in FOLDED for g in range(2)}
         early[2, 0] = sums(6, 2, g=0)
         second = {3: sums(5, 3, g=1)}
         early[1, 2] = sums(4, 1, g=2)
         third = {2: sums(7, 2, g=2)}
 
-        wc_dealt = wc_grouped[:].rearrange("p (t h m i) -> p h m i t", t=PACK, h=2, i=PACK)
-        nc.scalar.copy(out=wc_dealt[:, 0], in_=wc_raw[0].rearrange("p i (m t) -> p m i t", t=PACK))
+        wc_dealt = wc_grouped[:].rearrange("p (t m i) -> p m i t", t=PACK, i=PACK)
+        nc.scalar.copy(out=wc_dealt[:, : EARLY // PACK], in_=wc_raw[0].rearrange("p i (m t) -> p m i t", t=PACK))
         first_copy(0, early[0, 0])
-        nc.scalar.copy(out=wc_dealt[:, 1], in_=wc_raw[1].rearrange("p i (m t) -> p m i t", t=PACK))
+        nc.scalar.copy(out=wc_dealt[:, EARLY // PACK :], in_=wc_raw[1].rearrange("p i (m t) -> p m i t", t=PACK))
         nc.vector.quantize_mx(out=wc_codes[:].bitcast(FP8X4), scales=wc_plane[:], in_=wc_grouped[:])
         early[3, 0] = sums(0, 3, g=0)
         round_c(0)

from contextlib import ExitStack

import concourse.mybir as mybir
from concourse.masks import make_identity

K, R, N, T, J, G = 512, 512, 256, 4096, 512, 4
FLOPS = 2 * K * R * J * (G + 1) + 2 * R * N * J

F32 = mybir.dt.float32
BF16 = mybir.dt.bfloat16
I32 = mybir.dt.int32
U32 = mybir.dt.uint32
U16 = mybir.dt.uint16
U8 = mybir.dt.uint8
FP8X4 = mybir.dt.float8_e4m3fn_x4
FP4X4 = mybir.dt.float4_e2m1fn_x4
ACT = mybir.ActivationFunctionType
MAX = mybir.AluOpType.max
ADD = mybir.AluOpType.add
MULT = mybir.AluOpType.mult

P = 128
PACK = 4
TILES = J // P
FIRST_ROW = P - 16
WEIGHT_ROW = P // 2 - 16
FOLDED = (0, 1)
TURNED = (2, 3)
HALF = 4 * PACK * J // 2
PAD = HALF // 4
EARLY = 5 * R // 8


def columns(tile, width=P):
    return slice(tile * width, (tile + 1) * width)


def move_home(nc, plane, rows, first_row):
    for r in range(4):
        nc.sync.dma_start(out=plane[r:P:32, :].bitcast(I32), in_=rows[first_row + r : first_row + 16 : 4, :].bitcast(I32))


def tile_list_pnet_bias_kernel(
    tc, tab_words, tab_scales, c, w_words, w_scales, wc, wd_words, wd_scales, b, offs, out
):
    nc = tc.nc
    with ExitStack() as ctx:
        keep = ctx.enter_context(tc.tile_pool(name="keep", bufs=1))
        wc_side = ctx.enter_context(tc.tile_pool(name="wc_side", bufs=1))
        c_side = ctx.enter_context(tc.tile_pool(name="c_side", bufs=1))
        rounded = ctx.enter_context(tc.tile_pool(name="rounded", bufs=1))
        ending = ctx.enter_context(tc.tile_pool(name="ending", bufs=1))
        psum = ctx.enter_context(tc.psum_pool(name="psum", bufs=1))

        offsets = keep.tile([P, G * J // 16], U16, name="offsets")
        picked_rows = keep.tile([P, G * J], U8, name="picked_rows", align_bytes=64)
        table = keep.tile([P, T], I32, name="table", align_bytes=64)
        weight_rows = keep.tile([P, R + N], U8, name="weight_rows", align_bytes=64)
        weight_plane = keep.tile([P, R + N], U8, name="weight_plane", align_bytes=64)
        w_rows = wc_side.tile([P, R], U8, name="w_rows", align_bytes=64, offset=4 * PACK * EARLY - R // 2)
        late_raw = c_side.tile([P, PACK * J], F32, name="late_raw", align_bytes=64, offset=0)
        late = [late_raw[:, cols].rearrange("p (t j) -> p t j", t=PACK) for cols in (slice(0, PACK * (R - EARLY)), columns(1, PACK * J // 2))]
        wc_raw = [wc_side.tile([P, PACK, EARLY], F32, name="wc_raw0", align_bytes=64, offset=0)[:], late[0]]
        w_codes = wc_side.tile([P, R], U32, name="w_codes", align_bytes=64, offset=4 * PACK * EARLY)
        tab_rows = c_side.tile([P, T], U8, name="tab_rows", align_bytes=64, offset=2 * HALF - PAD // 4)
        wd_codes = c_side.tile([P, 2 * N], U8, name="wd_codes", align_bytes=64, offset=2 * HALF)
        bias = c_side.tile([P, N // P], F32, name="bias", align_bytes=64, offset=2 * HALF + 3 * N)
        c_start = [2 * HALF + PAD + G * J, 0]
        c_wide = c_side.tile([P, PACK * J // 2 + 16], F32, name="c_raw0", align_bytes=64, offset=c_start[0])
        c_raw = [c_wide[:, : PACK * J // 2].rearrange("p (t j) -> p t j", t=PACK), late[1]]

        identity = keep.tile([P, P], F32, name="identity", align_bytes=64)
        make_identity(nc, identity[:])
        nc.vector.memset(w_rows[:WEIGHT_ROW, :].bitcast(I32), 0)
        nc.vector.memset(w_rows[P // 2 :, :].bitcast(I32), 0)
        nc.vector.memset(tab_rows[:FIRST_ROW, :].bitcast(I32), 0)
        nc.vector.memset(weight_plane[:].bitcast(I32), 0)

        nc.scalar.dma_start(out=tab_rows[FIRST_ROW:, :].bitcast(I32), in_=tab_scales[0].bitcast(I32))
        nc.sync.dma_start(out=w_rows[WEIGHT_ROW : P // 2, :].bitcast(I32), in_=w_scales[0].bitcast(I32))
        nc.sync.dma_start(offsets[:], offs)
        nc.sync.dma_start(out=table[:], in_=tab_words[0].rearrange("p t i -> p (t i)").bitcast(I32))
        nc.scalar.dma_start(out=weight_rows[WEIGHT_ROW : P // 2, R:].bitcast(I32), in_=wd_scales[0].bitcast(I32))

        nc.vector.tensor_copy(weight_rows[:, :R].rearrange("p (t m) -> p t m", t=PACK), w_rows[:].rearrange("p (m t) -> p t m", t=PACK))
        move_home(nc, weight_plane, weight_rows, WEIGHT_ROW)
        nc.sync.dma_start(out=w_codes[:].bitcast(I32), in_=w_words[0].rearrange("p r i -> p (r i)").bitcast(I32))
        wc_rows = wc.rearrange("(p t) r -> p t r", t=PACK)
        nc.sync.dma_start(out=wc_raw[0], in_=wc_rows[:, :, :EARLY])

        nc.vector.tensor_copy(picked_rows[:], tab_rows[:].indirect(offsets[:]))
        picked_plane = c_side.tile([P, G * J], U8, name="picked_plane", align_bytes=64, offset=2 * HALF + PAD)
        move_home(nc, picked_plane, picked_rows, FIRST_ROW)
        nc.sync.dma_start(out=wc_raw[1], in_=wc_rows[:, :, EARLY:])
        c_rows = c.rearrange("(p t) j -> p t j", t=PACK)
        for h in range(2):
            nc.sync.dma_start(out=c_raw[h], in_=c_rows[:, :, columns(h, J // 2)])
        nc.sync.dma_start(out=wd_codes[:].bitcast(I32), in_=wd_words[0].bitcast(I32))
        with nc.allow_non_contiguous_dma(reason="one bias value a partition"):
            nc.sync.dma_start(out=bias[:], in_=b.rearrange("(h p) -> p h", p=P))

        def gather_words(tile, first, count):
            nc.vector.tensor_copy(tile[:], table[:].bitcast(U32).indirect(offsets[:, first * J // 16 : (first + count) * J // 16]))
            return [tile[:, columns(n, J)] for n in range(count)]

        picked = gather_words(keep.tile([P, J], U32, name="picked0", align_bytes=64), 0, 1)
        w_dealt = keep.tile([P, R], U32, name="w_dealt", align_bytes=64)
        nc.scalar.copy(
            out=w_dealt[:].rearrange("p (t m i) -> p m t i", t=PACK, i=4), in_=w_codes[:].rearrange("p (m i t) -> p m t i", t=PACK, i=4)
        )
        picked.extend(gather_words(keep.tile([P, J], U32, name="picked1", align_bytes=64), 1, 1))
        picked.extend(gather_words(keep.tile([P, 2 * J], U32, name="picked2", align_bytes=64), 2, 2))

        wc_grouped = keep.tile([P, PACK * R], BF16, name="wc_grouped", align_bytes=64)
        wc_codes = keep.tile([P, R], U32, name="wc_codes", align_bytes=64)
        wc_plane = keep.tile([P, R], U8, name="wc_plane", align_bytes=64)
        c_grouped = [rounded.tile([P, PACK * J // 2], BF16, name=f"c_grouped{h}", align_bytes=64, offset=0) for h in range(2)]
        c_codes = [keep.tile([P, J // 2], U32, name=f"c_codes{h}", align_bytes=64) for h in range(2)]
        c_plane = [keep.tile([P, J // 2], U8, name=f"c_plane{h}", align_bytes=64) for h in range(2)]

        def sums(index, unit, g=None, with_own=False):
            if unit in TURNED:
                bank = psum.tile([P, PACK, P], F32, name="bank", tag=f"bank{index}")
                if with_own:
                    moving, moving_plane, codes, plane = wc_codes[:], wc_plane[:], c_codes[1][:, columns(unit % 2)], c_plane[1][:, columns(unit % 2)]
                else:
                    moving, moving_plane = w_dealt[:], weight_plane[:, :R]
                    codes, plane = picked[g][:, columns(unit)], picked_plane[:, columns(g * TILES + unit)]
                nc.tensor.matmul_mx(
                    out=bank[:].rearrange("p t m -> p (t m)"), lhsT=codes.bitcast(FP8X4), lhsT_scale=plane,
                    rhs=moving.bitcast(FP8X4), rhs_scale=moving_plane, start=True, stop=True,
                )
                return bank[:]
            bank = psum.tile([P, 2, 2 * P], F32, name="bank", tag=f"bank{index}")
            passes = []
            if g is not None:
                passes.append((w_dealt[:], weight_plane[:, :R], picked[g][:, : 2 * P], picked_plane[:, columns(2 * g, 2 * P)]))
            if with_own:
                passes.append((wc_codes[:], wc_plane[:], c_codes[0][:], c_plane[0][:]))
            for n, (codes, plane, moving, moving_plane) in enumerate(passes):
                for e in range(2):
                    t = 2 * unit + e
                    nc.tensor.matmul_mx(
                        out=bank[:, e, :], lhsT=codes[:, columns(t)].bitcast(FP8X4), lhsT_scale=plane[:, columns(t)],
                        rhs=moving.bitcast(FP8X4), rhs_scale=moving_plane,
                        start=n == 0 and e == 0, stop=n == len(passes) - 1 and e == 1,
                    )
            return bank[:].rearrange("p e j -> p j e")

        def layout(unit):
            return [P, PACK, P] if unit in TURNED else [P, 2 * P, 2]

        def round_c(h):
            nc.scalar.copy(
                out=c_grouped[h][:].rearrange("p (j i t) -> p j t i", i=4, t=PACK),
                in_=c_raw[h].rearrange("p t (j i) -> p j t i", i=4),
            )

        def quantise_c(h):
            nc.vector.quantize_mx(out=c_codes[h][:].bitcast(FP8X4), scales=c_plane[h][:], in_=c_grouped[h][:])

        pooled = {}

        def first_copy(jt, bank):
            if jt == 0:
                pooled[jt] = keep.tile(layout(jt), F32, name="pooled0", align_bytes=64)
            else:
                start = c_start[0] + (jt - 1) * HALF // 2
                pooled[jt] = c_side.tile(layout(jt), F32, name=f"pooled{jt}", align_bytes=64, offset=start)
            nc.scalar.copy(out=pooled[jt][:], in_=bank)

        def maximum(jt, bank):
            nc.vector.tensor_tensor(out=pooled[jt][:], in0=pooled[jt][:], in1=bank, op=MAX)

        own = {}

        def own_copy(jt, bank):
            own[jt] = keep.tile(layout(jt), F32, name=f"own{jt}", align_bytes=64)
            nc.scalar.copy(out=own[jt][:], in_=bank)

        early = {(jt, g): sums(2 * g + jt, jt, g=g) for jt in FOLDED for g in range(2)}
        early[2, 0] = sums(6, 2, g=0)
        second = {3: sums(5, 3, g=1)}
        early[1, 2] = sums(4, 1, g=2)
        third = {2: sums(7, 2, g=2)}

        wc_dealt = wc_grouped[:].rearrange("p (t m i) -> p m i t", t=PACK, i=PACK)
        nc.scalar.copy(out=wc_dealt[:, : EARLY // PACK], in_=wc_raw[0].rearrange("p i (m t) -> p m i t", t=PACK))
        first_copy(0, early[0, 0])
        nc.scalar.copy(out=wc_dealt[:, EARLY // PACK :], in_=wc_raw[1].rearrange("p i (m t) -> p m i t", t=PACK))
        nc.vector.quantize_mx(out=wc_codes[:].bitcast(FP8X4), scales=wc_plane[:], in_=wc_grouped[:])
        early[3, 0] = sums(0, 3, g=0)
        round_c(0)
        first_copy(1, early[1, 0])
        maximum(0, early[0, 1])
        second[2] = sums(2, 2, g=1)
        quantise_c(0)
        nc.gpsimd.tensor_scalar(
            c_grouped[1][:].rearrange("p (j t) -> p j t", t=PACK), c_raw[1].rearrange("p t j -> p j t"), 1.0, 0.0, op0=MULT, op1=ADD
        )
        own_banks = (3, 6)
        early[0, 2] = sums(1, 0, g=2)
        maximum(1, early[1, 1])
        for jt in TURNED:
            first_copy(jt, early[jt, 0])
        for jt in FOLDED:
            own_copy(jt, sums(own_banks[jt], jt, with_own=True))
        third[3] = sums(0, 3, g=2)
        for jt in FOLDED:
            maximum(jt, early[jt, 2])
        quantise_c(1)
        three = rounded.tile([P, 2, 2 * P, 2], BF16, name="three", align_bytes=64, offset=0)
        for jt in FOLDED:
            nc.gpsimd.tensor_tensor(out=three[:, jt], in0=pooled[jt][:], in1=own[jt][:], op=ADD)
        folded = {}
        for jt in TURNED:
            own_copy(jt, sums(own_banks[jt - 2], jt, with_own=True))
        for jt in TURNED:
            maximum(jt, second[jt])
        fourth = {}
        for jt in FOLDED:
            folded[jt] = sums((1, 4)[jt], jt, g=3, with_own=True)
            fourth[jt + 2] = sums((2, 5)[jt], jt + 2, g=3)
        last = keep.tile([P, 2, 2 * P, 2], BF16, name="last", align_bytes=64)
        for jt in FOLDED:
            nc.scalar.activation(out=last[:, jt], in_=folded[jt], func=ACT.Relu)
        summed = {}
        for jt in TURNED:
            summed[jt] = psum.tile([P, PACK, P], F32, name="bank", tag=f"bank{own_banks[jt - 2]}")
            for t in range(PACK):
                nc.tensor.matmul(summed[jt][:, t, :], own[jt][:, t, :], identity[:], start=t == 0, stop=False, is_transpose=True)
        for jt in TURNED:
            maximum(jt, third[jt])

        h_grouped = [ending.tile([P, 2, P, PACK], BF16, name=f"h_grouped{h}", align_bytes=64, offset=h * HALF // 2) for h in range(2)]
        h_codes = keep.tile([P, J], U32, name="h_codes", align_bytes=64)
        h_plane = keep.tile([P, J], U8, name="h_plane", align_bytes=64)
        for jt in TURNED:
            for half in range(2):
                slots = slice(2 * half, 2 * half + 2)
                nc.vector.tensor_tensor(out=pooled[jt][:, slots], in0=pooled[jt][:, slots], in1=fourth[jt][:, slots], op=MAX)
                for t in range(2 * half, 2 * half + 2):
                    nc.tensor.matmul(summed[jt][:, t, :], pooled[jt][:, t, :], identity[:], start=False, stop=t == PACK - 1, is_transpose=True)
            nc.scalar.activation(out=h_grouped[1][:, jt - 2], in_=summed[jt][:].rearrange("p t j -> p j t"), func=ACT.Relu)
        for jt in FOLDED:
            nc.vector.tensor_tensor(
                out=h_grouped[0][:, jt].rearrange("p j (u e) -> p j u e", e=2),
                in0=last[:, :, columns(jt), :].rearrange("p u j e -> p j u e"),
                in1=three[:, :, columns(jt), :].rearrange("p u j e -> p j u e"),
                op=MAX,
            )

        def quantise(first_tile, count):
            cols = slice(first_tile * P, (first_tile + count) * P)
            source = h_grouped[first_tile // 2][:, first_tile % 2 : first_tile % 2 + count]
            nc.vector.quantize_mx(out=h_codes[:, cols].bitcast(FP8X4), scales=h_plane[:, cols], in_=source.rearrange("p a j t -> p (a j t)"))

        out_rows = out.rearrange("(h p) j -> p h j", p=P)

        def second_layer(target, h, cols):
            nc.tensor.matmul_mx(
                out=target, lhsT=wd_codes[:, columns(h, 2 * P)].bitcast(FP4X4), lhsT_scale=weight_plane[:, R + h * P : R + (h + 1) * P],
                rhs=h_codes[:, cols].bitcast(FP8X4), rhs_scale=h_plane[:, cols], start=True, stop=True,
            )

        def add_bias_scalar(result, y, h):
            nc.scalar.activation(out=result, in_=y, func=ACT.Identity, bias=bias[:, h : h + 1])

        def add_bias_vector(result, y, h):
            nc.vector.tensor_scalar(result, y, bias[:, h : h + 1], None, op0=ADD)

        for jt in range(TILES):
            quantise(jt, 1)
        for h in range(2):
            y = psum.tile([P, 2 * P], F32, name="bank", tag=f"bank{(1, 4)[h]}")
            second_layer(y[:], h, columns(0, 2 * P))
            result = keep.tile([P, 2 * P], F32, name=f"result{h}", align_bytes=64)
            add_bias_scalar(result[:], y[:], h)
            nc.sync.dma_start(out=out_rows[:, h, columns(0, 2 * P)], in_=result[:])
        results = {
            2: ending.tile([P, 2, P], F32, name="result2", align_bytes=64, offset=HALF // 2),
            3: keep.tile([P, 2, P], F32, name="result3", align_bytes=64),
        }
        for jt, add_bias, queue in ((2, add_bias_vector, nc.sync), (3, add_bias_scalar, nc.scalar)):
            y = psum.tile([P, 2, P], F32, name="bank", tag=f"bank{(7, 0)[jt - 2]}")
            for h in range(2):
                second_layer(y[:, h], h, columns(jt))
            for h in range(2):
                add_bias(results[jt][:, h], y[:, h], h)
            queue.dma_start(out=out_rows[:, :, columns(jt)], in_=results[jt][:])
